import numpy as np
import ml_dtypes


def mxq(x, axis, fmt="e4m3"):
    dtype, down = {"e4m3": (ml_dtypes.float8_e4m3fn, 7), "e5m2": (ml_dtypes.float8_e5m2, 14)}[fmt]
    v = np.moveaxis(np.asarray(x, np.float32).astype(ml_dtypes.bfloat16).astype(np.float64), axis, -1)
    blocks = v.reshape(v.shape[:-1] + (-1, 32))
    amax = np.abs(blocks).max(-1, keepdims=True)
    byte = np.maximum(np.where(amax > 0, np.frexp(amax)[1] - 1 + 127, 0) - down, 1)
    scale = np.exp2(byte - 127.0)
    codes = (blocks / scale).astype(np.float32).astype(dtype).astype(np.float64)
    return np.moveaxis((codes * scale).reshape(v.shape), -1, axis)


WIDE = False


def mx_kscale(k):
    if not WIDE:
        return np.ones(k)
    levels = np.array([10, -10, 5, -5, 0])
    if k % 512:
        return np.exp2(np.random.permutation(np.resize(levels, k // 32))).repeat(32)
    a = np.empty((k // 512, 16))
    for p in range(k // 512):
        a[p, :8] = np.random.permutation(np.resize(levels, 8))
        for g in range(8):
            far = levels[np.abs(levels - a[p, g]) >= 10]
            a[p, g + 8] = far[np.random.randint(len(far))]
    return np.exp2(a.ravel()).repeat(32)


def f64(x):
    return np.asarray(x).astype(np.float64)


def striped(idx):
    return np.tile(idx.reshape(-1, 16).T, (8, 1)).astype(np.uint16)


def unstriped(offs):
    return offs[:16].T.reshape(-1).astype(np.int64)


def pack_weight(w):
    k, n = w.shape
    w = f64(np.asarray(w, np.float32).astype(ml_dtypes.bfloat16)).reshape(k // 32, 32, n)
    amax = np.abs(w).max(1)
    byte = np.clip(np.where(amax > 0, np.frexp(amax)[1] - 1 + 127 - 7, 1), 1, 254)
    scaled = (w * np.exp2(127.0 - byte)[:, None, :]).reshape(k, n).astype(np.float32)
    words = np.ascontiguousarray(scaled.reshape(k // 512, 128, 4, n).transpose(0, 1, 3, 2)).astype(ml_dtypes.float8_e4m3fn).view(np.uint8)
    return words, np.ascontiguousarray(byte.astype(np.uint8).reshape(k // 512, 16, n))


def unpack_weight(words, scales):
    g, p, n, _ = words.shape
    vals = np.ascontiguousarray(words).view(ml_dtypes.float8_e4m3fn).astype(np.float64) * np.repeat(np.exp2(scales.astype(np.float64) - 127.0), 8, axis=1)[..., None]
    return vals.transpose(0, 1, 3, 2).reshape(g * 512, n)


def silu(v):
    return v / (1.0 + np.exp(-np.maximum(v, -700.0)))


K, T, S, H, N = 1024, 2048, 1024, 512, 256


def setup_inputs():
    n = np.random.standard_normal
    s = mx_kscale(K)[:, None]
    u = mx_kscale(H)
    packed_xT = pack_weight(n((K, T)) * s)
    packed_w2 = pack_weight(n((H, N)) / np.sqrt(2 * H) / u[:, None])
    packed_w3 = pack_weight(n((K, N)) / np.sqrt(2 * K) / s)
    return {
        "x_words": packed_xT[0],
        "x_scales": packed_xT[1],
        "w1": (n((K, H)) / np.sqrt(K) / s * u).astype(np.float32),
        "w2_words": packed_w2[0],
        "w2_scales": packed_w2[1],
        "w3_words": packed_w3[0],
        "w3_scales": packed_w3[1],
        "offs": striped(np.random.permutation(T)[:S]),
    }


def reference(x_words, x_scales, w1, w2_words, w2_scales, w3_words, w3_scales, offs):
    xq = unpack_weight(x_words, x_scales)[:, unstriped(offs)]
    h = silu(mxq(f64(w1), 0, "e4m3").T @ xq)
    return unpack_weight(w2_words, w2_scales).T @ mxq(h, 0, "e4m3") + unpack_weight(w3_words, w3_scales).T @ xq

@@ -1,0 +1,197 @@
+from contextlib import ExitStack
+
+import concourse.mybir as mybir
+
+K, T, S, H, N = 1024, 2048, 1024, 512, 256
+FLOPS = 2 * S * (K * H + H * N + K * N)
+
+F32 = mybir.dt.float32
+BF16 = mybir.dt.bfloat16
+I32 = mybir.dt.int32
+U32 = mybir.dt.uint32
+U16 = mybir.dt.uint16
+U8 = mybir.dt.uint8
+FP8X4 = mybir.dt.float8_e4m3fn_x4
+SILU = mybir.ActivationFunctionType.Silu
+
+P = 128
+PACK = 4
+PASSES = K // (P * PACK)
+QUADS = 4
+BANK = 128
+GATHER = 256
+HALF = H // 2
+
+
+def tile_picked_zskip_silu_p_kernel(
+    tc, x_words, x_scales, w1, w2_words, w2_scales, w3_words, w3_scales, offs, out
+):
+    nc = tc.nc
+    with ExitStack() as ctx:
+        keep = ctx.enter_context(tc.tile_pool(name="keep", bufs=1))
+        psum = ctx.enter_context(tc.psum_pool(name="psum", bufs=1))
+
+        def sb(name, shape, dtype, tag=""):
+            return keep.tile(shape, dtype, name=name, tag=tag, align_bytes=64)
+
+        offsets = sb("offsets", [P, S // 16], U16)
+        xs_table = sb("xs_table", [P, T], U8, "slot_d")
+        ws = sb("ws", [P, N], U8)
+        warm = sb("warm", [P, 8], F32, "slot_b")
+        warm_out = sb("warm_out", [P, 8], BF16, "slot_c")
+        nc.vector.memset(xs_table[:].bitcast(I32), 0)
+        nc.gpsimd.memset(ws[:].bitcast(I32), 0)
+        nc.vector.memset(warm[:], 0.0)
+        nc.scalar.activation(warm_out[:], warm[:], SILU)
+
+        w1_bf = [sb("w1_bf%d" % g, [P, PACK, P, PACK], BF16, "slot_bf%d" % g) for g in range(PASSES)]
+        w1_codes = [sb("w1_codes%d" % g, [P, H], U32) for g in range(PASSES)]
+        w1_scales = [sb("w1_scales%d" % g, [P, H], U8) for g in range(PASSES)]
+
+        def load_w1(g, u, tag):
+            raw = sb("w1_raw%d%d" % (g, u), [P, PACK, HALF], F32, tag)
+            rows = w1[512 * g : 512 * (g + 1), HALF * u : HALF * (u + 1)]
+            nc.sync.dma_start(raw[:], rows.rearrange("(p j) c -> p j c", j=PACK))
+            return raw
+
+        def cast_w1(g, u, raw):
+            dst = w1_bf[g][:].rearrange("p t m j -> p m t j")[:, 64 * u : 64 * (u + 1)]
+            nc.scalar.copy(dst, raw[:].rearrange("p j (m t) -> p m t j", t=PACK))
+
+        def load_x(g, tag):
+            table = sb("x_table%d" % g, [P, T], I32, tag)
+            nc.sync.dma_start(table[:], x_words[g].rearrange("p n t -> p (n t)").bitcast(I32))
+            return table
+
+        def quantize_w1(g):
+            nc.vector.quantize_mx(
+                out=w1_codes[g][:].bitcast(FP8X4),
+                scales=w1_scales[g][:],
+                in_=w1_bf[g][:].rearrange("p t m j -> p (t m j)"),
+            )
+
+        nc.sync.dma_start(offsets[:], offs)
+        raw00 = load_w1(0, 0, "slot_a")
+        for q in range(QUADS):
+            nc.sync.dma_start(
+                xs_table[32 * q : 32 * q + 8, :].bitcast(I32), x_scales[:, 4 * q : 4 * q + 4, :].bitcast(I32)
+            )
+        raw01 = load_w1(0, 1, "slot_b")
+        x_table0 = load_x(0, "slot_c")
+        for q in range(QUADS):
+            nc.gpsimd.dma_start(
+                ws[32 * q : 32 * q + 8, :].bitcast(I32), w3_scales[:, 4 * q : 4 * q + 4, :].bitcast(I32)
+            )
+        for q in range(QUADS):
+            nc.gpsimd.dma_start(
+                ws[32 * q + 8 : 32 * q + 12, :].bitcast(I32), w2_scales[0, 4 * q : 4 * q + 4, :].bitcast(I32)
+            )
+        cast_w1(0, 0, raw00)
+        raw10 = load_w1(1, 0, "slot_a")
+        cast_w1(0, 1, raw01)
+        raw11 = load_w1(1, 1, "slot_b")
+
+        xs = sb("xs", [P, S], U8)
+        nc.vector.tensor_copy(xs[:], xs_table[:].indirect(offsets[:]))
+        x_table1 = load_x(1, "slot_d")
+        x_table = [x_table0, x_table1]
+
+        banks = [psum.tile([P, 512], F32, name="h%d" % b, tag="bank%d" % b) for b in range(8)]
+        x_codes = []
+
+        def gather(g, c):
+            cols = slice(GATHER * c, GATHER * (c + 1))
+            nc.vector.tensor_copy(
+                x_codes[g][:, cols], x_table[g][:].bitcast(U32).indirect(offsets[:, 16 * c : 16 * (c + 1)])
+            )
+
+        def first(g, b):
+            cols = slice(BANK * b, BANK * (b + 1))
+            for t in range(PACK):
+                m = slice(P * t, P * (t + 1))
+                nc.tensor.matmul_mx(
+                    out=banks[b][:, m],
+                    lhsT=w1_codes[g][:, m].bitcast(FP8X4),
+                    lhsT_scale=w1_scales[g][:, m],
+                    rhs=x_codes[g][:, cols].bitcast(FP8X4),
+                    rhs_scale=xs[4 * g : P, cols],
+                    start=(g == 0 and t == 0),
+                    stop=(g == PASSES - 1 and t == PACK - 1),
+                )
+
+        chunks = [(0, 256, (0,)), (256, 256, (1,)), (512, 256, (2,)), (768, 128, (3,)), (896, 128, (4, 5))]
+        h_bf = sb("h_bf", [P, S, PACK], BF16)
+        h_codes = sb("h_codes", [P, S], U32)
+        h_scales = sb("h_scales", [P, S], U8)
+
+        def silu(b):
+            nc.scalar.activation(
+                h_bf[:, BANK * b : BANK * (b + 1), :], banks[b][:].rearrange("p (t n) -> p n t", t=PACK), SILU
+            )
+
+        quantize_w1(0)
+        x_codes.append(sb("x_codes0", [P, S], U32, "slot_bf0"))
+        for c in range(S // GATHER):
+            gather(0, c)
+            first(0, 2 * c)
+            first(0, 2 * c + 1)
+        w23 = sb("w23", [P, PASSES + 1, N], I32, "slot_c")
+        nc.sync.dma_start(w23[:, :PASSES, :], w3_words.rearrange("g p n t -> p g (n t)").bitcast(I32))
+        nc.sync.dma_start(w23[:, PASSES, :], w2_words[0].rearrange("p n t -> p (n t)").bitcast(I32))
+        cast_w1(1, 0, raw10)
+        cast_w1(1, 1, raw11)
+        quantize_w1(1)
+        x_codes.append(sb("x_codes1", [P, S], U32, "slot_bf1"))
+        for c in range(S // GATHER):
+            gather(1, c)
+            for b in (2 * c, 2 * c + 1):
+                first(1, b)
+                silu(b)
+
+        out_v = out.rearrange("(m p) n -> p m n", p=P)
+        for c, (c0, width, use) in enumerate(chunks):
+            cols = slice(c0, c0 + width)
+            tiles = [psum.tile([P, 512], F32, name="o%d_%d" % (c, b), tag="bank%d" % b) for b in use]
+            split = len(use) == 2
+            acc = [tiles[m][:, :width] if split else tiles[0][:, width * m : width * (m + 1)] for m in range(2)]
+            res = sb("res%d" % c, [P, 2, width], F32)
+            for m in range(2):
+                mc = slice(P * m, P * (m + 1))
+                for g in range(PASSES):
+                    nc.tensor.matmul_mx(
+                        out=acc[m],
+                        lhsT=w23[:, g, mc].bitcast(FP8X4),
+                        lhsT_scale=ws[4 * g : P, mc],
+                        rhs=x_codes[g][:, cols].bitcast(FP8X4),
+                        rhs_scale=xs[4 * g : P, cols],
+                        start=(g == 0 and (split or m == 0)),
+                        stop=False,
+                    )
+            nc.vector.quantize_mx(
+                out=h_codes[:, cols].bitcast(FP8X4),
+                scales=h_scales[:, cols],
+                in_=h_bf[:, cols, :].rearrange("p n t -> p (n t)"),
+            )
+            for m in range(2):
+                mc = slice(P * m, P * (m + 1))
+                nc.tensor.matmul_mx(
+                    out=acc[m],
+                    lhsT=w23[:, PASSES, mc].bitcast(FP8X4),
+                    lhsT_scale=ws[8:P, mc],
+                    rhs=h_codes[:, cols].bitcast(FP8X4),
+                    rhs_scale=h_scales[:, cols],
+                    start=False,
+                    stop=(split or m == 1),
+                )
+            if split:
+                nc.vector.tensor_copy(res[:, 0, :], acc[0])
+                nc.sync.dma_start(out_v[:, 0, cols], res[:, 0, :])
+                nc.scalar.copy(res[:, 1, :], acc[1])
+                nc.scalar.dma_start(out_v[:, 1, cols], res[:, 1, :])
+            else:
+                both = tiles[0][:, : 2 * width].rearrange("p (m n) -> p m n", m=2)
+                if c == len(chunks) - 2:
+                    nc.scalar.copy(res[:], both)
+                else:
+                    nc.vector.tensor_copy(res[:], both)
+                nc.sync.dma_start(out_v[:, :, cols], res[:])

@@ -20,7 +20,7 @@ PASSES = K // (P * PACK)
 QUADS = 4
 BANK = 128
 GATHER = 256
-HALF = H // 2
+V_SHARE = (48, 72)
 
 
 def tile_picked_zskip_silu_p_kernel(
@@ -29,6 +29,7 @@ def tile_picked_zskip_silu_p_kernel(
     nc = tc.nc
     with ExitStack() as ctx:
         keep = ctx.enter_context(tc.tile_pool(name="keep", bufs=1))
+        tables = ctx.enter_context(tc.tile_pool(name="tables", bufs=1))
         psum = ctx.enter_context(tc.psum_pool(name="psum", bufs=1))
 
         def sb(name, shape, dtype, tag=""):
@@ -37,29 +38,32 @@ def tile_picked_zskip_silu_p_kernel(
         offsets = sb("offsets", [P, S // 16], U16)
         xs_table = sb("xs_table", [P, T], U8, "slot_d")
         ws = sb("ws", [P, N], U8)
-        warm = sb("warm", [P, 8], F32, "slot_b")
-        warm_out = sb("warm_out", [P, 8], BF16, "slot_c")
+        w1_raw = sb("w1_raw", [P, PASSES * PACK * H], F32)
+        warm = tables.tile([P, 16], F32, name="warm", offset=4 * T - 32)
+        warm_out = w1_raw[:, PACK * H - 8 : PACK * H + 8]
         nc.vector.memset(xs_table[:].bitcast(I32), 0)
         nc.gpsimd.memset(ws[:].bitcast(I32), 0)
         nc.vector.memset(warm[:], 0.0)
-        nc.scalar.activation(warm_out[:], warm[:], SILU)
+        nc.scalar.activation(warm_out, warm[:], SILU)
 
         w1_bf = [sb("w1_bf%d" % g, [P, PACK, P, PACK], BF16, "slot_bf%d" % g) for g in range(PASSES)]
         w1_codes = [sb("w1_codes%d" % g, [P, H], U32) for g in range(PASSES)]
         w1_scales = [sb("w1_scales%d" % g, [P, H], U8) for g in range(PASSES)]
 
-        def load_w1(g, u, tag):
-            raw = sb("w1_raw%d%d" % (g, u), [P, PACK, HALF], F32, tag)
-            rows = w1[512 * g : 512 * (g + 1), HALF * u : HALF * (u + 1)]
-            nc.sync.dma_start(raw[:], rows.rearrange("(p j) c -> p j c", j=PACK))
-            return raw
+        w1_rows = w1_raw[:].rearrange("p (g j c) -> p g j c", g=PASSES, j=PACK)
 
-        def cast_w1(g, u, raw):
-            dst = w1_bf[g][:].rearrange("p t m j -> p m t j")[:, 64 * u : 64 * (u + 1)]
-            nc.scalar.copy(dst, raw[:].rearrange("p j (m t) -> p m t j", t=PACK))
+        def load_w1(g, j0, j1):
+            rows = w1[512 * g : 512 * (g + 1), :].rearrange("(p j) c -> p j c", j=PACK)
+            nc.sync.dma_start(w1_rows[:, g, j0:j1], rows[:, j0:j1])
 
-        def load_x(g, tag):
-            table = sb("x_table%d" % g, [P, T], I32, tag)
+        def cast_w1(g):
+            dst = w1_bf[g][:].rearrange("p t m j -> p m j t")
+            src = w1_rows[:, g].rearrange("p j (m t) -> p m j t", t=PACK)
+            nc.scalar.copy(dst[:, V_SHARE[g] :], src[:, V_SHARE[g] :])
+            nc.vector.tensor_copy(dst[:, : V_SHARE[g]], src[:, : V_SHARE[g]])
+
+        def load_x(g):
+            table = tables.tile([P, T], I32, name="x_table%d" % g, offset=4 * T * g)
             nc.sync.dma_start(table[:], x_words[g].rearrange("p n t -> p (n t)").bitcast(I32))
             return table
 
@@ -70,14 +74,16 @@ def tile_picked_zskip_silu_p_kernel(
                 in_=w1_bf[g][:].rearrange("p t m j -> p (t m j)"),
             )
 
+        load_w1(0, 0, 2)
         nc.sync.dma_start(offsets[:], offs)
-        raw00 = load_w1(0, 0, "slot_a")
         for q in range(QUADS):
             nc.sync.dma_start(
                 xs_table[32 * q : 32 * q + 8, :].bitcast(I32), x_scales[:, 4 * q : 4 * q + 4, :].bitcast(I32)
             )
-        raw01 = load_w1(0, 1, "slot_b")
-        x_table0 = load_x(0, "slot_c")
+        load_w1(0, 2, 4)
+        x_table0 = load_x(0)
+        load_w1(1, 0, 4)
+        x_table1 = load_x(1)
         for q in range(QUADS):
             nc.gpsimd.dma_start(
                 ws[32 * q : 32 * q + 8, :].bitcast(I32), w3_scales[:, 4 * q : 4 * q + 4, :].bitcast(I32)
@@ -86,14 +92,9 @@ def tile_picked_zskip_silu_p_kernel(
             nc.gpsimd.dma_start(
                 ws[32 * q + 8 : 32 * q + 12, :].bitcast(I32), w2_scales[0, 4 * q : 4 * q + 4, :].bitcast(I32)
             )
-        cast_w1(0, 0, raw00)
-        raw10 = load_w1(1, 0, "slot_a")
-        cast_w1(0, 1, raw01)
-        raw11 = load_w1(1, 1, "slot_b")
-
         xs = sb("xs", [P, S], U8)
         nc.vector.tensor_copy(xs[:], xs_table[:].indirect(offsets[:]))
-        x_table1 = load_x(1, "slot_d")
+        cast_w1(0)
         x_table = [x_table0, x_table1]
 
         banks = [psum.tile([P, 512], F32, name="h%d" % b, tag="bank%d" % b) for b in range(8)]
@@ -119,14 +120,17 @@ def tile_picked_zskip_silu_p_kernel(
                     stop=(g == PASSES - 1 and t == PACK - 1),
                 )
 
-        chunks = [(0, 256, (0,)), (256, 256, (1,)), (512, 256, (2,)), (768, 128, (3,)), (896, 128, (4, 5))]
-        h_bf = sb("h_bf", [P, S, PACK], BF16)
+        chunks = [(0, 256, (0,)), (256, 256, (3,)), (512, 256, (4, 5)), (768, 128, (6,)), (896, 128, (1, 2))]
+        h_bf = [sb("h_bf%d" % c, [P, width, PACK], BF16, "slot_h%d" % c) for c, (c0, width, use) in enumerate(chunks)]
+        res_slot = ["slot_h1", "slot_h2", "slot_h3", "res3", "res4"]
         h_codes = sb("h_codes", [P, S], U32)
         h_scales = sb("h_scales", [P, S], U8)
 
         def silu(b):
+            c = max(i for i, chunk in enumerate(chunks) if chunk[0] <= BANK * b)
+            n0 = BANK * b - chunks[c][0]
             nc.scalar.activation(
-                h_bf[:, BANK * b : BANK * (b + 1), :], banks[b][:].rearrange("p (t n) -> p n t", t=PACK), SILU
+                h_bf[c][:, n0 : n0 + BANK, :], banks[b][:].rearrange("p (t n) -> p n t", t=PACK), SILU
             )
 
         quantize_w1(0)
@@ -135,11 +139,10 @@ def tile_picked_zskip_silu_p_kernel(
             gather(0, c)
             first(0, 2 * c)
             first(0, 2 * c + 1)
-        w23 = sb("w23", [P, PASSES + 1, N], I32, "slot_c")
+        w23 = sb("w23", [P, PASSES + 1, N], I32, "slot_d")
         nc.sync.dma_start(w23[:, :PASSES, :], w3_words.rearrange("g p n t -> p g (n t)").bitcast(I32))
         nc.sync.dma_start(w23[:, PASSES, :], w2_words[0].rearrange("p n t -> p (n t)").bitcast(I32))
-        cast_w1(1, 0, raw10)
-        cast_w1(1, 1, raw11)
+        cast_w1(1)
         quantize_w1(1)
         x_codes.append(sb("x_codes1", [P, S], U32, "slot_bf1"))
         for c in range(S // GATHER):
@@ -148,13 +151,21 @@ def tile_picked_zskip_silu_p_kernel(
                 first(1, b)
                 silu(b)
 
+        for c, (c0, width, use) in enumerate(chunks):
+            cols = slice(c0, c0 + width)
+            nc.vector.quantize_mx(
+                out=h_codes[:, cols].bitcast(FP8X4),
+                scales=h_scales[:, cols],
+                in_=h_bf[c][:].rearrange("p n t -> p (n t)"),
+            )
+
         out_v = out.rearrange("(m p) n -> p m n", p=P)
         for c, (c0, width, use) in enumerate(chunks):
             cols = slice(c0, c0 + width)
             tiles = [psum.tile([P, 512], F32, name="o%d_%d" % (c, b), tag="bank%d" % b) for b in use]
             split = len(use) == 2
             acc = [tiles[m][:, :width] if split else tiles[0][:, width * m : width * (m + 1)] for m in range(2)]
-            res = sb("res%d" % c, [P, 2, width], F32)
+            res = sb("res%d" % c, [P, 2, width], F32, res_slot[c])
             for m in range(2):
                 mc = slice(P * m, P * (m + 1))
                 for g in range(PASSES):
@@ -167,11 +178,6 @@ def tile_picked_zskip_silu_p_kernel(
                         start=(g == 0 and (split or m == 0)),
                         stop=False,
                     )
-            nc.vector.quantize_mx(
-                out=h_codes[:, cols].bitcast(FP8X4),
-                scales=h_scales[:, cols],
-                in_=h_bf[:, cols, :].rearrange("p n t -> p (n t)"),
-            )
             for m in range(2):
                 mc = slice(P * m, P * (m + 1))
                 nc.tensor.matmul_mx(
@@ -183,7 +189,11 @@ def tile_picked_zskip_silu_p_kernel(
                     start=False,
                     stop=(split or m == 1),
                 )
-            if split:
+            if split and c < len(chunks) - 1:
+                nc.vector.tensor_copy(res[:, 0, :], acc[0])
+                nc.scalar.copy(res[:, 1, :], acc[1])
+                nc.sync.dma_start(out_v[:, :, cols], res[:])
+            elif split:
                 nc.vector.tensor_copy(res[:, 0, :], acc[0])
                 nc.sync.dma_start(out_v[:, 0, cols], res[:, 0, :])
                 nc.scalar.copy(res[:, 1, :], acc[1])

@@ -20,7 +20,7 @@ PASSES = K // (P * PACK)
 QUADS = 4
 BANK = 128
 GATHER = 256
-V_SHARE = (48, 72)
+V_SHARE = (56, 72)
 
 
 def tile_picked_zskip_silu_p_kernel(
@@ -46,7 +46,7 @@ def tile_picked_zskip_silu_p_kernel(
         nc.vector.memset(warm[:], 0.0)
         nc.scalar.activation(warm_out, warm[:], SILU)
 
-        w1_bf = [sb("w1_bf%d" % g, [P, PACK, P, PACK], BF16, "slot_bf%d" % g) for g in range(PASSES)]
+        w1_bf = [sb("w1_bf%d" % g, [P, PACK, P, PACK], BF16) for g in range(PASSES)]
         w1_codes = [sb("w1_codes%d" % g, [P, H], U32) for g in range(PASSES)]
         w1_scales = [sb("w1_scales%d" % g, [P, H], U8) for g in range(PASSES)]
 
@@ -120,9 +120,9 @@ def tile_picked_zskip_silu_p_kernel(
                     stop=(g == PASSES - 1 and t == PACK - 1),
                 )
 
-        chunks = [(0, 256, (0,)), (256, 256, (3,)), (512, 256, (4, 5)), (768, 128, (6,)), (896, 128, (1, 2))]
+        chunks = [(0, 256, (0,)), (256, 256, (3,)), (512, 256, (5,)), (768, 256, (1, 6))]
         h_bf = [sb("h_bf%d" % c, [P, width, PACK], BF16, "slot_h%d" % c) for c, (c0, width, use) in enumerate(chunks)]
-        res_slot = ["slot_h1", "slot_h2", "slot_h3", "res3", "res4"]
+        res_slot = ["slot_h1", "slot_h2", "res2", "res3"]
         h_codes = sb("h_codes", [P, S], U32)
         h_scales = sb("h_scales", [P, S], U8)
 
@@ -134,7 +134,7 @@ def tile_picked_zskip_silu_p_kernel(
             )
 
         quantize_w1(0)
-        x_codes.append(sb("x_codes0", [P, S], U32, "slot_bf0"))
+        x_codes.append(sb("x_codes0", [P, S], U32))
         for c in range(S // GATHER):
             gather(0, c)
             first(0, 2 * c)
@@ -144,7 +144,7 @@ def tile_picked_zskip_silu_p_kernel(
         nc.sync.dma_start(w23[:, PASSES, :], w2_words[0].rearrange("p n t -> p (n t)").bitcast(I32))
         cast_w1(1)
         quantize_w1(1)
-        x_codes.append(sb("x_codes1", [P, S], U32, "slot_bf1"))
+        x_codes.append(sb("x_codes1", [P, S], U32))
         for c in range(S // GATHER):
             gather(1, c)
             for b in (2 * c, 2 * c + 1):

@@ -20,7 +20,7 @@ PASSES = K // (P * PACK)
 QUADS = 4
 BANK = 128
 GATHER = 256
-V_SHARE = (56, 72)
+V_SHARE = (44, 72)
 
 
 def tile_picked_zskip_silu_p_kernel(
@@ -46,7 +46,7 @@ def tile_picked_zskip_silu_p_kernel(
         nc.vector.memset(warm[:], 0.0)
         nc.scalar.activation(warm_out, warm[:], SILU)
 
-        w1_bf = [sb("w1_bf%d" % g, [P, PACK, P, PACK], BF16) for g in range(PASSES)]
+        w1_bf = [sb("w1_bf%d" % g, [P, PACK, P, PACK], BF16, "slot_bf%d" % g) for g in range(PASSES)]
         w1_codes = [sb("w1_codes%d" % g, [P, H], U32) for g in range(PASSES)]
         w1_scales = [sb("w1_scales%d" % g, [P, H], U8) for g in range(PASSES)]
 
@@ -88,10 +88,6 @@ def tile_picked_zskip_silu_p_kernel(
             nc.gpsimd.dma_start(
                 ws[32 * q : 32 * q + 8, :].bitcast(I32), w3_scales[:, 4 * q : 4 * q + 4, :].bitcast(I32)
             )
-        for q in range(QUADS):
-            nc.gpsimd.dma_start(
-                ws[32 * q + 8 : 32 * q + 12, :].bitcast(I32), w2_scales[0, 4 * q : 4 * q + 4, :].bitcast(I32)
-            )
         xs = sb("xs", [P, S], U8)
         nc.vector.tensor_copy(xs[:], xs_table[:].indirect(offsets[:]))
         cast_w1(0)
@@ -120,7 +116,7 @@ def tile_picked_zskip_silu_p_kernel(
                     stop=(g == PASSES - 1 and t == PACK - 1),
                 )
 
-        chunks = [(0, 256, (0,)), (256, 256, (3,)), (512, 256, (5,)), (768, 256, (1, 6))]
+        chunks = [(0, 256, (0,)), (256, 256, (3,)), (512, 256, (4, 5)), (768, 256, (1, 7))]
         h_bf = [sb("h_bf%d" % c, [P, width, PACK], BF16, "slot_h%d" % c) for c, (c0, width, use) in enumerate(chunks)]
         res_slot = ["slot_h1", "slot_h2", "res2", "res3"]
         h_codes = sb("h_codes", [P, S], U32)
@@ -142,6 +138,12 @@ def tile_picked_zskip_silu_p_kernel(
         w23 = sb("w23", [P, PASSES + 1, N], I32, "slot_d")
         nc.sync.dma_start(w23[:, :PASSES, :], w3_words.rearrange("g p n t -> p g (n t)").bitcast(I32))
         nc.sync.dma_start(w23[:, PASSES, :], w2_words[0].rearrange("p n t -> p (n t)").bitcast(I32))
+        w2s = sb("w2s", [P, N], U8, "slot_bf0")
+        nc.gpsimd.memset(w2s[:].bitcast(I32), 0)
+        for q in range(QUADS):
+            nc.scalar.dma_start(
+                w2s[32 * q : 32 * q + 4, :].bitcast(I32), w2_scales[0, 4 * q : 4 * q + 4, :].bitcast(I32)
+            )
         cast_w1(1)
         quantize_w1(1)
         x_codes.append(sb("x_codes1", [P, S], U32))
@@ -183,7 +185,7 @@ def tile_picked_zskip_silu_p_kernel(
                 nc.tensor.matmul_mx(
                     out=acc[m],
                     lhsT=w23[:, PASSES, mc].bitcast(FP8X4),
-                    lhsT_scale=ws[8:P, mc],
+                    lhsT_scale=w2s[:, mc],
                     rhs=h_codes[:, cols].bitcast(FP8X4),
                     rhs_scale=h_scales[:, cols],
                     start=False,

@@ -33,11 +33,14 @@ def tile_picked_zskip_silu_p_kernel(
         psum = ctx.enter_context(tc.psum_pool(name="psum", bufs=1))
 
         def sb(name, shape, dtype, tag=""):
-            return keep.tile(shape, dtype, name=name, tag=tag, align_bytes=64)
+            return keep.tile(shape, dtype, name=name, tag=tag, align_bytes=256)
+
+        def shifted(name, width, dtype, lead, tag=""):
+            return sb(name, [P, lead + width], dtype, tag)[:, lead:]
 
         offsets = sb("offsets", [P, S // 16], U16)
         xs_table = sb("xs_table", [P, T], U8, "slot_d")
-        ws = sb("ws", [P, N], U8)
+        ws = shifted("ws", N, U8, 64)
         w1_raw = sb("w1_raw", [P, PASSES * PACK * H], F32)
         warm = tables.tile([P, 16], F32, name="warm", offset=4 * T - 32)
         warm_out = w1_raw[:, PACK * H - 8 : PACK * H + 8]
@@ -48,7 +51,7 @@ def tile_picked_zskip_silu_p_kernel(
 
         w1_bf = [sb("w1_bf%d" % g, [P, PACK, P, PACK], BF16, "slot_bf%d" % g) for g in range(PASSES)]
         w1_codes = [sb("w1_codes%d" % g, [P, H], U32) for g in range(PASSES)]
-        w1_scales = [sb("w1_scales%d" % g, [P, H], U8) for g in range(PASSES)]
+        w1_scales = [shifted("w1_scales%d" % g, H, U8, 64) for g in range(PASSES)]
 
         w1_rows = w1_raw[:].rearrange("p (g j c) -> p g j c", g=PASSES, j=PACK)
 
@@ -88,7 +91,7 @@ def tile_picked_zskip_silu_p_kernel(
             nc.gpsimd.dma_start(
                 ws[32 * q : 32 * q + 8, :].bitcast(I32), w3_scales[:, 4 * q : 4 * q + 4, :].bitcast(I32)
             )
-        xs = sb("xs", [P, S], U8)
+        xs = shifted("xs", S, U8, 192)
         nc.vector.tensor_copy(xs[:], xs_table[:].indirect(offsets[:]))
         cast_w1(0)
         x_table = [x_table0, x_table1]
@@ -119,8 +122,8 @@ def tile_picked_zskip_silu_p_kernel(
         chunks = [(0, 256, (0,)), (256, 256, (3,)), (512, 256, (4, 5)), (768, 256, (1, 7))]
         h_bf = [sb("h_bf%d" % c, [P, width, PACK], BF16, "slot_h%d" % c) for c, (c0, width, use) in enumerate(chunks)]
         res_slot = ["slot_h1", "slot_h2", "res2", "res3"]
-        h_codes = sb("h_codes", [P, S], U32)
-        h_scales = sb("h_scales", [P, S], U8)
+        h_codes = shifted("h_codes", S, U32, 32)
+        h_scales = shifted("h_scales", S, U8, 192)
 
         def silu(b):
             c = max(i for i, chunk in enumerate(chunks) if chunk[0] <= BANK * b)
@@ -130,7 +133,7 @@ def tile_picked_zskip_silu_p_kernel(
             )
 
         quantize_w1(0)
-        x_codes.append(sb("x_codes0", [P, S], U32))
+        x_codes.append(shifted("x_codes0", S, U32, 32))
         for c in range(S // GATHER):
             gather(0, c)
             first(0, 2 * c)
@@ -138,7 +141,7 @@ def tile_picked_zskip_silu_p_kernel(
         w23 = sb("w23", [P, PASSES + 1, N], I32, "slot_d")
         nc.sync.dma_start(w23[:, :PASSES, :], w3_words.rearrange("g p n t -> p g (n t)").bitcast(I32))
         nc.sync.dma_start(w23[:, PASSES, :], w2_words[0].rearrange("p n t -> p (n t)").bitcast(I32))
-        w2s = sb("w2s", [P, N], U8, "slot_bf0")
+        w2s = shifted("w2s", N, U8, 64, "slot_bf0")
         nc.gpsimd.memset(w2s[:].bitcast(I32), 0)
         for q in range(QUADS):
             nc.scalar.dma_start(
@@ -146,7 +149,7 @@ def tile_picked_zskip_silu_p_kernel(
             )
         cast_w1(1)
         quantize_w1(1)
-        x_codes.append(sb("x_codes1", [P, S], U32))
+        x_codes.append(shifted("x_codes1", S, U32, 32))
         for c in range(S // GATHER):
             gather(1, c)
             for b in (2 * c, 2 * c + 1):

@@ -77,12 +77,18 @@ def tile_picked_zskip_silu_p_kernel(
                 in_=w1_bf[g][:].rearrange("p t m j -> p (t m j)"),
             )
 
-        load_w1(0, 0, 2)
         nc.sync.dma_start(offsets[:], offs)
-        for q in range(QUADS):
+        load_w1(0, 0, 2)
+        for q in range(QUADS // 2):
             nc.sync.dma_start(
                 xs_table[32 * q : 32 * q + 8, :].bitcast(I32), x_scales[:, 4 * q : 4 * q + 4, :].bitcast(I32)
             )
+        for q in range(QUADS // 2, QUADS):
+            for g in range(PASSES):
+                first_row = 32 * q + 4 * g
+                nc.sync.dma_start(
+                    xs_table[first_row : first_row + 4, :].bitcast(I32), x_scales[g, 4 * q : 4 * q + 4, :].bitcast(I32)
+                )
         load_w1(0, 2, 4)
         x_table0 = load_x(0)
         load_w1(1, 0, 4)

@@ -20,7 +20,8 @@ PASSES = K // (P * PACK)
 QUADS = 4
 BANK = 128
 GATHER = 256
-V_SHARE = (44, 72)
+V_SHARE = (48, 68)
+FIRST = 768
 
 
 def tile_picked_zskip_silu_p_kernel(
@@ -42,12 +43,12 @@ def tile_picked_zskip_silu_p_kernel(
         xs_table = sb("xs_table", [P, T], U8, "slot_d")
         ws = shifted("ws", N, U8, 64)
         w1_raw = sb("w1_raw", [P, PASSES * PACK * H], F32)
-        warm = tables.tile([P, 16], F32, name="warm", offset=4 * T - 32)
-        warm_out = w1_raw[:, PACK * H - 8 : PACK * H + 8]
+        warm_out = tables.tile([P, 16], F32, name="warm_out", offset=4 * T - 32)
+        warm = w1_raw[:, PACK * H - 8 : PACK * H + 16]
         nc.vector.memset(xs_table[:].bitcast(I32), 0)
         nc.gpsimd.memset(ws[:].bitcast(I32), 0)
-        nc.vector.memset(warm[:], 0.0)
-        nc.scalar.activation(warm_out, warm[:], SILU)
+        nc.vector.memset(warm, 0.0)
+        nc.scalar.activation(warm_out[:], warm[:, 8:], SILU)
 
         w1_bf = [sb("w1_bf%d" % g, [P, PACK, P, PACK], BF16, "slot_bf%d" % g) for g in range(PASSES)]
         w1_codes = [sb("w1_codes%d" % g, [P, H], U32) for g in range(PASSES)]
@@ -55,9 +56,9 @@ def tile_picked_zskip_silu_p_kernel(
 
         w1_rows = w1_raw[:].rearrange("p (g j c) -> p g j c", g=PASSES, j=PACK)
 
-        def load_w1(g, j0, j1):
-            rows = w1[512 * g : 512 * (g + 1), :].rearrange("(p j) c -> p j c", j=PACK)
-            nc.sync.dma_start(w1_rows[:, g, j0:j1], rows[:, j0:j1])
+        def load_w1(g, c0, c1):
+            rows = w1[512 * g : 512 * (g + 1), :].rearrange("(p j) c -> p (j c)", j=PACK)
+            nc.sync.dma_start(w1_raw[:, PACK * H * g + c0 : PACK * H * g + c1], rows[:, c0:c1])
 
         def cast_w1(g):
             dst = w1_bf[g][:].rearrange("p t m j -> p m j t")
@@ -78,7 +79,7 @@ def tile_picked_zskip_silu_p_kernel(
             )
 
         nc.sync.dma_start(offsets[:], offs)
-        load_w1(0, 0, 2)
+        load_w1(0, 0, FIRST)
         for q in range(QUADS // 2):
             nc.sync.dma_start(
                 xs_table[32 * q : 32 * q + 8, :].bitcast(I32), x_scales[:, 4 * q : 4 * q + 4, :].bitcast(I32)
@@ -89,9 +90,9 @@ def tile_picked_zskip_silu_p_kernel(
                 nc.sync.dma_start(
                     xs_table[first_row : first_row + 4, :].bitcast(I32), x_scales[g, 4 * q : 4 * q + 4, :].bitcast(I32)
                 )
-        load_w1(0, 2, 4)
+        load_w1(0, FIRST, PACK * H)
         x_table0 = load_x(0)
-        load_w1(1, 0, 4)
+        load_w1(1, 0, PACK * H)
         x_table1 = load_x(1)
         for q in range(QUADS):
             nc.gpsimd.dma_start(

@@ -201,15 +201,10 @@ def tile_picked_zskip_silu_p_kernel(
                     start=False,
                     stop=(split or m == 1),
                 )
-            if split and c < len(chunks) - 1:
+            if split:
                 nc.vector.tensor_copy(res[:, 0, :], acc[0])
                 nc.scalar.copy(res[:, 1, :], acc[1])
                 nc.sync.dma_start(out_v[:, :, cols], res[:])
-            elif split:
-                nc.vector.tensor_copy(res[:, 0, :], acc[0])
-                nc.sync.dma_start(out_v[:, 0, cols], res[:, 0, :])
-                nc.scalar.copy(res[:, 1, :], acc[1])
-                nc.scalar.dma_start(out_v[:, 1, cols], res[:, 1, :])
             else:
                 both = tiles[0][:, : 2 * width].rearrange("p (m n) -> p m n", m=2)
                 if c == len(chunks) - 2:

@@ -20,8 +20,9 @@ PASSES = K // (P * PACK)
 QUADS = 4
 BANK = 128
 GATHER = 256
-V_SHARE = (48, 68)
+V_SHARE = (76, 68)
 FIRST = 768
+ROW0 = 96
 
 
 def tile_picked_zskip_silu_p_kernel(
@@ -30,7 +31,6 @@ def tile_picked_zskip_silu_p_kernel(
     nc = tc.nc
     with ExitStack() as ctx:
         keep = ctx.enter_context(tc.tile_pool(name="keep", bufs=1))
-        tables = ctx.enter_context(tc.tile_pool(name="tables", bufs=1))
         psum = ctx.enter_context(tc.psum_pool(name="psum", bufs=1))
 
         def sb(name, shape, dtype, tag=""):
@@ -40,15 +40,19 @@ def tile_picked_zskip_silu_p_kernel(
             return sb(name, [P, lead + width], dtype, tag)[:, lead:]
 
         offsets = sb("offsets", [P, S // 16], U16)
-        xs_table = sb("xs_table", [P, T], U8, "slot_d")
+        xs_table = sb("xs_table", [P, T], U8)
+        xs_picked = sb("xs_picked", [P, S], U8)
+        xs_both = shifted("xs", PASSES * S, U8, 192)
+        xs = [xs_both[:, S * g : S * (g + 1)] for g in range(PASSES)]
         ws = shifted("ws", N, U8, 64)
         w1_raw = sb("w1_raw", [P, PASSES * PACK * H], F32)
-        warm_out = tables.tile([P, 16], F32, name="warm_out", offset=4 * T - 32)
-        warm = w1_raw[:, PACK * H - 8 : PACK * H + 16]
-        nc.vector.memset(xs_table[:].bitcast(I32), 0)
+        warm = sb("warm", [P, 16], F32)
+        warm_out = sb("warm_out", [P, 16], F32)
+        nc.vector.memset(warm[:], 0.0)
+        nc.scalar.activation(warm_out[:], warm[:], SILU)
+        nc.vector.memset(xs_table[:ROW0, :].bitcast(I32), 0)
+        nc.vector.memset(xs_both[:].bitcast(I32), 0)
         nc.gpsimd.memset(ws[:].bitcast(I32), 0)
-        nc.vector.memset(warm, 0.0)
-        nc.scalar.activation(warm_out[:], warm[:, 8:], SILU)
 
         w1_bf = [sb("w1_bf%d" % g, [P, PACK, P, PACK], BF16, "slot_bf%d" % g) for g in range(PASSES)]
         w1_codes = [sb("w1_codes%d" % g, [P, H], U32) for g in range(PASSES)]
@@ -67,7 +71,7 @@ def tile_picked_zskip_silu_p_kernel(
             nc.vector.tensor_copy(dst[:, : V_SHARE[g]], src[:, : V_SHARE[g]])
 
         def load_x(g):
-            table = tables.tile([P, T], I32, name="x_table%d" % g, offset=4 * T * g)
+            table = sb("x_table%d" % g, [P, T], I32)
             nc.sync.dma_start(table[:], x_words[g].rearrange("p n t -> p (n t)").bitcast(I32))
             return table
 
@@ -78,28 +82,33 @@ def tile_picked_zskip_silu_p_kernel(
                 in_=w1_bf[g][:].rearrange("p t m j -> p (t m j)"),
             )
 
+        def place_scales(g):
+            for q in range(QUADS):
+                src = ROW0 + 16 * g + 4 * q
+                dst = 32 * q + 4 * g
+                nc.sync.dma_start(xs[g][dst : dst + 4, :].bitcast(I32), xs_picked[src : src + 4, :].bitcast(I32))
+
         nc.sync.dma_start(offsets[:], offs)
-        load_w1(0, 0, FIRST)
-        for q in range(QUADS // 2):
-            nc.sync.dma_start(
-                xs_table[32 * q : 32 * q + 8, :].bitcast(I32), x_scales[:, 4 * q : 4 * q + 4, :].bitcast(I32)
-            )
-        for q in range(QUADS // 2, QUADS):
-            for g in range(PASSES):
-                first_row = 32 * q + 4 * g
-                nc.sync.dma_start(
-                    xs_table[first_row : first_row + 4, :].bitcast(I32), x_scales[g, 4 * q : 4 * q + 4, :].bitcast(I32)
-                )
-        load_w1(0, FIRST, PACK * H)
+        nc.sync.dma_start(xs_table[ROW0:, :].bitcast(I32), x_scales.rearrange("g q n -> (g q) n").bitcast(I32))
+        load_w1(0, 0, PACK * H)
         x_table0 = load_x(0)
-        load_w1(1, 0, PACK * H)
-        x_table1 = load_x(1)
         for q in range(QUADS):
             nc.gpsimd.dma_start(
                 ws[32 * q : 32 * q + 8, :].bitcast(I32), w3_scales[:, 4 * q : 4 * q + 4, :].bitcast(I32)
             )
-        xs = shifted("xs", S, U8, 192)
-        nc.vector.tensor_copy(xs[:], xs_table[:].indirect(offsets[:]))
+        for q in range(QUADS):
+            nc.gpsimd.dma_start(
+                ws[32 * q + 8 : 32 * q + 12, :].bitcast(I32), w2_scales[0, 4 * q : 4 * q + 4, :].bitcast(I32)
+            )
+        nc.vector.tensor_copy(xs_picked[:], xs_table[:].indirect(offsets[:]))
+        load_w1(1, 0, FIRST)
+        place_scales(0)
+        load_w1(1, FIRST, PACK * H)
+        x_table1 = load_x(1)
+        place_scales(1)
+        w23 = sb("w23", [P, PASSES + 1, N], I32)
+        nc.sync.dma_start(w23[:, :PASSES, :], w3_words.rearrange("g p n t -> p g (n t)").bitcast(I32))
+        nc.sync.dma_start(w23[:, PASSES, :], w2_words[0].rearrange("p n t -> p (n t)").bitcast(I32))
         cast_w1(0)
         x_table = [x_table0, x_table1]
 
@@ -121,7 +130,7 @@ def tile_picked_zskip_silu_p_kernel(
                     lhsT=w1_codes[g][:, m].bitcast(FP8X4),
                     lhsT_scale=w1_scales[g][:, m],
                     rhs=x_codes[g][:, cols].bitcast(FP8X4),
-                    rhs_scale=xs[4 * g : P, cols],
+                    rhs_scale=xs[g][4 * g : P, cols],
                     start=(g == 0 and t == 0),
                     stop=(g == PASSES - 1 and t == PACK - 1),
                 )
@@ -145,15 +154,6 @@ def tile_picked_zskip_silu_p_kernel(
             gather(0, c)
             first(0, 2 * c)
             first(0, 2 * c + 1)
-        w23 = sb("w23", [P, PASSES + 1, N], I32, "slot_d")
-        nc.sync.dma_start(w23[:, :PASSES, :], w3_words.rearrange("g p n t -> p g (n t)").bitcast(I32))
-        nc.sync.dma_start(w23[:, PASSES, :], w2_words[0].rearrange("p n t -> p (n t)").bitcast(I32))
-        w2s = shifted("w2s", N, U8, 64, "slot_bf0")
-        nc.gpsimd.memset(w2s[:].bitcast(I32), 0)
-        for q in range(QUADS):
-            nc.scalar.dma_start(
-                w2s[32 * q : 32 * q + 4, :].bitcast(I32), w2_scales[0, 4 * q : 4 * q + 4, :].bitcast(I32)
-            )
         cast_w1(1)
         quantize_w1(1)
         x_codes.append(shifted("x_codes1", S, U32, 32))
@@ -186,7 +186,7 @@ def tile_picked_zskip_silu_p_kernel(
                         lhsT=w23[:, g, mc].bitcast(FP8X4),
                         lhsT_scale=ws[4 * g : P, mc],
                         rhs=x_codes[g][:, cols].bitcast(FP8X4),
-                        rhs_scale=xs[4 * g : P, cols],
+                        rhs_scale=xs[g][4 * g : P, cols],
                         start=(g == 0 and (split or m == 0)),
                         stop=False,
                     )
@@ -195,7 +195,7 @@ def tile_picked_zskip_silu_p_kernel(
                 nc.tensor.matmul_mx(
                     out=acc[m],
                     lhsT=w23[:, PASSES, mc].bitcast(FP8X4),
-                    lhsT_scale=w2s[:, mc],
+                    lhsT_scale=ws[8:P, mc],
                     rhs=h_codes[:, cols].bitcast(FP8X4),
                     rhs_scale=h_scales[:, cols],
                     start=False,

@@ -20,9 +20,10 @@ PASSES = K // (P * PACK)
 QUADS = 4
 BANK = 128
 GATHER = 256
-V_SHARE = (76, 68)
-FIRST = 768
+V_SHARE = (76, 80)
+FIRST = 640
 ROW0 = 96
+PLANE = (12, 4)
 
 
 def tile_picked_zskip_silu_p_kernel(
@@ -83,9 +84,11 @@ def tile_picked_zskip_silu_p_kernel(
             )
 
         def place_scales(g):
-            for q in range(QUADS):
+            for q in (0, 2, 1, 3):
                 src = ROW0 + 16 * g + 4 * q
-                dst = 32 * q + 4 * g
+                dst = 32 * q + PLANE[g]
+                if src == dst:
+                    continue
                 nc.sync.dma_start(xs[g][dst : dst + 4, :].bitcast(I32), xs_picked[src : src + 4, :].bitcast(I32))
 
         nc.sync.dma_start(offsets[:], offs)
@@ -130,7 +133,7 @@ def tile_picked_zskip_silu_p_kernel(
                     lhsT=w1_codes[g][:, m].bitcast(FP8X4),
                     lhsT_scale=w1_scales[g][:, m],
                     rhs=x_codes[g][:, cols].bitcast(FP8X4),
-                    rhs_scale=xs[g][4 * g : P, cols],
+                    rhs_scale=xs[g][PLANE[g] : P, cols],
                     start=(g == 0 and t == 0),
                     stop=(g == PASSES - 1 and t == PACK - 1),
                 )
@@ -149,6 +152,7 @@ def tile_picked_zskip_silu_p_kernel(
             )
 
         quantize_w1(0)
+        nc.vector.tensor_copy(xs[0][ROW0:, :].bitcast(I32), xs_picked[ROW0:, :].bitcast(I32))
         x_codes.append(shifted("x_codes0", S, U32, 32))
         for c in range(S // GATHER):
             gather(0, c)
@@ -186,7 +190,7 @@ def tile_picked_zskip_silu_p_kernel(
                         lhsT=w23[:, g, mc].bitcast(FP8X4),
                         lhsT_scale=ws[4 * g : P, mc],
                         rhs=x_codes[g][:, cols].bitcast(FP8X4),
-                        rhs_scale=xs[g][4 * g : P, cols],
+                        rhs_scale=xs[g][PLANE[g] : P, cols],
                         start=(g == 0 and (split or m == 0)),
                         stop=False,
                     )

@@ -138,9 +138,9 @@ def tile_picked_zskip_silu_p_kernel(
                     stop=(g == PASSES - 1 and t == PACK - 1),
                 )
 
-        chunks = [(0, 256, (0,)), (256, 256, (3,)), (512, 256, (4, 5)), (768, 256, (1, 7))]
+        chunks = [(0, 256, (0,)), (256, 256, (3,)), (512, 256, (4, 5)), (768, 128, (6,)), (896, 128, (1, 7))]
         h_bf = [sb("h_bf%d" % c, [P, width, PACK], BF16, "slot_h%d" % c) for c, (c0, width, use) in enumerate(chunks)]
-        res_slot = ["slot_h1", "slot_h2", "res2", "res3"]
+        res_slot = ["slot_h1", "slot_h2", "res2", "res3", "res4"]
         h_codes = shifted("h_codes", S, U32, 32)
         h_scales = shifted("h_scales", S, U8, 192)
 

@@ -16,14 +16,28 @@ SILU = mybir.ActivationFunctionType.Silu
 
 P = 128
 PACK = 4
-PASSES = K // (P * PACK)
+PASS_K = P * PACK
+PASSES = K // PASS_K
 QUADS = 4
-BANK = 128
+QUAD = P // QUADS
+QUAD_ROWS = 4
+PLANE_ROWS = QUADS * QUAD_ROWS
+LIST_ROWS = 16
+BANKS = 8
+BANK_COLS = 512
+BANK_TOKENS = S // BANKS
 GATHER = 256
-V_SHARE = (76, 80)
-FIRST = 640
-ROW0 = 96
-PLANE = (12, 4)
+HALVES = N // P
+
+VECTOR_SHARE = (76, 80)
+W1_LEAD = 640
+TABLE_ROW0 = P - QUAD
+X_PLANE = (12, 4)
+BANKS_BEFORE_SHORTCUT = 6
+LEAD_STATIONARY_SCALES, LEAD_MOVING_CODES, LEAD_MOVING_SCALES = 64, 128, 192
+
+CHUNKS = ((0, 256, (0,)), (256, 256, (3,)), (512, 256, (4, 5)), (768, 128, (6,)), (896, 128, (1, 7)))
+H_COL0 = (0, 256, 512, 256, 896)
 
 
 def tile_picked_zskip_silu_p_kernel(
@@ -34,47 +48,46 @@ def tile_picked_zskip_silu_p_kernel(
         keep = ctx.enter_context(tc.tile_pool(name="keep", bufs=1))
         psum = ctx.enter_context(tc.psum_pool(name="psum", bufs=1))
 
-        def sb(name, shape, dtype, tag=""):
-            return keep.tile(shape, dtype, name=name, tag=tag, align_bytes=256)
+        def sb(name, shape, dtype):
+            return keep.tile(shape, dtype, name=name, align_bytes=256)
 
-        def shifted(name, width, dtype, lead, tag=""):
-            return sb(name, [P, lead + width], dtype, tag)[:, lead:]
+        def bytes_at(name, width, lead):
+            return sb(name, [P, lead + width], U8)[:, lead:]
 
-        offsets = sb("offsets", [P, S // 16], U16)
+        def words_at(name, width, lead):
+            return sb(name, [P, lead // PACK + width], U32)[:, lead // PACK :]
+
+        offsets = sb("offsets", [P, S // LIST_ROWS], U16)
         xs_table = sb("xs_table", [P, T], U8)
         xs_picked = sb("xs_picked", [P, S], U8)
-        xs_both = shifted("xs", PASSES * S, U8, 192)
-        xs = [xs_both[:, S * g : S * (g + 1)] for g in range(PASSES)]
-        ws = shifted("ws", N, U8, 64)
+        xs_planes = bytes_at("xs_planes", PASSES * S, LEAD_MOVING_SCALES)
+        xs = [xs_planes[:, S * g : S * (g + 1)] for g in range(PASSES)]
+        ws = bytes_at("ws", 2 * N, LEAD_STATIONARY_SCALES)
         w1_raw = sb("w1_raw", [P, PASSES * PACK * H], F32)
+
         warm = sb("warm", [P, 16], F32)
         warm_out = sb("warm_out", [P, 16], F32)
         nc.vector.memset(warm[:], 0.0)
         nc.scalar.activation(warm_out[:], warm[:], SILU)
-        nc.vector.memset(xs_table[:ROW0, :].bitcast(I32), 0)
-        nc.vector.memset(xs_both[:].bitcast(I32), 0)
+
+        nc.vector.memset(xs_table[:TABLE_ROW0, :].bitcast(I32), 0)
+        nc.vector.memset(xs_planes[:].bitcast(I32), 0)
         nc.gpsimd.memset(ws[:].bitcast(I32), 0)
 
-        w1_bf = [sb("w1_bf%d" % g, [P, PACK, P, PACK], BF16, "slot_bf%d" % g) for g in range(PASSES)]
+        w1_bf = [sb("w1_bf%d" % g, [P, PACK, P, PACK], BF16) for g in range(PASSES)]
         w1_codes = [sb("w1_codes%d" % g, [P, H], U32) for g in range(PASSES)]
-        w1_scales = [shifted("w1_scales%d" % g, H, U8, 64) for g in range(PASSES)]
-
+        w1_scales = [bytes_at("w1_scales%d" % g, H, LEAD_STATIONARY_SCALES) for g in range(PASSES)]
         w1_rows = w1_raw[:].rearrange("p (g j c) -> p g j c", g=PASSES, j=PACK)
 
-        def load_w1(g, c0, c1):
-            rows = w1[512 * g : 512 * (g + 1), :].rearrange("(p j) c -> p (j c)", j=PACK)
-            nc.sync.dma_start(w1_raw[:, PACK * H * g + c0 : PACK * H * g + c1], rows[:, c0:c1])
+        def load_w1(g, v0, v1):
+            rows = w1[PASS_K * g : PASS_K * (g + 1), :].rearrange("(p j) c -> p (j c)", j=PACK)
+            nc.sync.dma_start(w1_raw[:, PACK * H * g + v0 : PACK * H * g + v1], rows[:, v0:v1])
 
-        def cast_w1(g):
+        def round_w1(g):
             dst = w1_bf[g][:].rearrange("p t m j -> p m j t")
             src = w1_rows[:, g].rearrange("p j (m t) -> p m j t", t=PACK)
-            nc.scalar.copy(dst[:, V_SHARE[g] :], src[:, V_SHARE[g] :])
-            nc.vector.tensor_copy(dst[:, : V_SHARE[g]], src[:, : V_SHARE[g]])
-
-        def load_x(g):
-            table = sb("x_table%d" % g, [P, T], I32)
-            nc.sync.dma_start(table[:], x_words[g].rearrange("p n t -> p (n t)").bitcast(I32))
-            return table
+            nc.scalar.copy(dst[:, VECTOR_SHARE[g] :], src[:, VECTOR_SHARE[g] :])
+            nc.vector.tensor_copy(dst[:, : VECTOR_SHARE[g]], src[:, : VECTOR_SHARE[g]])
 
         def quantize_w1(g):
             nc.vector.quantize_mx(
@@ -83,136 +96,170 @@ def tile_picked_zskip_silu_p_kernel(
                 in_=w1_bf[g][:].rearrange("p t m j -> p (t m j)"),
             )
 
-        def place_scales(g):
+        def load_x(g):
+            table = sb("x_table%d" % g, [P, T], I32)
+            nc.sync.dma_start(table[:], x_words[g].rearrange("p n t -> p (n t)").bitcast(I32))
+            return table
+
+        def move_scales(g):
             for q in (0, 2, 1, 3):
-                src = ROW0 + 16 * g + 4 * q
-                dst = 32 * q + PLANE[g]
-                if src == dst:
-                    continue
-                nc.sync.dma_start(xs[g][dst : dst + 4, :].bitcast(I32), xs_picked[src : src + 4, :].bitcast(I32))
+                src = TABLE_ROW0 + PLANE_ROWS * g + QUAD_ROWS * q
+                dst = QUAD * q + X_PLANE[g]
+                if src != dst:
+                    nc.sync.dma_start(
+                        xs[g][dst : dst + QUAD_ROWS, :].bitcast(I32), xs_picked[src : src + QUAD_ROWS, :].bitcast(I32)
+                    )
 
         nc.sync.dma_start(offsets[:], offs)
-        nc.sync.dma_start(xs_table[ROW0:, :].bitcast(I32), x_scales.rearrange("g q n -> (g q) n").bitcast(I32))
+        nc.sync.dma_start(xs_table[TABLE_ROW0:, :].bitcast(I32), x_scales.rearrange("g q n -> (g q) n").bitcast(I32))
         load_w1(0, 0, PACK * H)
-        x_table0 = load_x(0)
+        x_table = [load_x(0)]
         for q in range(QUADS):
+            rows = slice(QUAD_ROWS * q, QUAD_ROWS * (q + 1))
             nc.gpsimd.dma_start(
-                ws[32 * q : 32 * q + 8, :].bitcast(I32), w3_scales[:, 4 * q : 4 * q + 4, :].bitcast(I32)
+                ws[QUAD * q : QUAD * q + PASSES * QUAD_ROWS, :N].bitcast(I32), w3_scales[:, rows, :].bitcast(I32)
             )
         for q in range(QUADS):
-            nc.gpsimd.dma_start(
-                ws[32 * q + 8 : 32 * q + 12, :].bitcast(I32), w2_scales[0, 4 * q : 4 * q + 4, :].bitcast(I32)
-            )
+            rows = slice(QUAD_ROWS * q, QUAD_ROWS * (q + 1))
+            nc.gpsimd.dma_start(ws[QUAD * q : QUAD * q + QUAD_ROWS, N:].bitcast(I32), w2_scales[0, rows, :].bitcast(I32))
         nc.vector.tensor_copy(xs_picked[:], xs_table[:].indirect(offsets[:]))
-        load_w1(1, 0, FIRST)
-        place_scales(0)
-        load_w1(1, FIRST, PACK * H)
-        x_table1 = load_x(1)
-        place_scales(1)
+        load_w1(1, 0, W1_LEAD)
+        move_scales(0)
+        load_w1(1, W1_LEAD, PACK * H)
+        x_table.append(load_x(1))
+        move_scales(1)
         w23 = sb("w23", [P, PASSES + 1, N], I32)
         nc.sync.dma_start(w23[:, :PASSES, :], w3_words.rearrange("g p n t -> p g (n t)").bitcast(I32))
         nc.sync.dma_start(w23[:, PASSES, :], w2_words[0].rearrange("p n t -> p (n t)").bitcast(I32))
-        cast_w1(0)
-        x_table = [x_table0, x_table1]
 
-        banks = [psum.tile([P, 512], F32, name="h%d" % b, tag="bank%d" % b) for b in range(8)]
+        round_w1(0)
+        hidden = [psum.tile([P, BANK_COLS], F32, name="h%d" % b, tag="bank%d" % b) for b in range(BANKS)]
+        h_bf = [sb("h_bf%d" % c, [P, width, PACK], BF16) for c, (tok0, width, banks) in enumerate(CHUNKS)]
+        h_codes = words_at("h_codes", S, LEAD_MOVING_CODES)
+        h_scales = bytes_at("h_scales", S, LEAD_MOVING_SCALES)
         x_codes = []
 
-        def gather(g, c):
-            cols = slice(GATHER * c, GATHER * (c + 1))
+        def gather_words(g, i):
+            entries = offsets[:, GATHER // LIST_ROWS * i : GATHER // LIST_ROWS * (i + 1)]
             nc.vector.tensor_copy(
-                x_codes[g][:, cols], x_table[g][:].bitcast(U32).indirect(offsets[:, 16 * c : 16 * (c + 1)])
+                x_codes[g][:, GATHER * i : GATHER * (i + 1)], x_table[g][:].bitcast(U32).indirect(entries)
             )
 
-        def first(g, b):
-            cols = slice(BANK * b, BANK * (b + 1))
+        def hidden_pass(g, b):
+            tokens = slice(BANK_TOKENS * b, BANK_TOKENS * (b + 1))
             for t in range(PACK):
-                m = slice(P * t, P * (t + 1))
+                tile_cols = slice(P * t, P * (t + 1))
                 nc.tensor.matmul_mx(
-                    out=banks[b][:, m],
-                    lhsT=w1_codes[g][:, m].bitcast(FP8X4),
-                    lhsT_scale=w1_scales[g][:, m],
-                    rhs=x_codes[g][:, cols].bitcast(FP8X4),
-                    rhs_scale=xs[g][PLANE[g] : P, cols],
+                    out=hidden[b][:, tile_cols],
+                    lhsT=w1_codes[g][:, tile_cols].bitcast(FP8X4),
+                    lhsT_scale=w1_scales[g][:, tile_cols],
+                    rhs=x_codes[g][:, tokens].bitcast(FP8X4),
+                    rhs_scale=xs[g][X_PLANE[g] : P, tokens],
                     start=(g == 0 and t == 0),
                     stop=(g == PASSES - 1 and t == PACK - 1),
                 )
 
-        chunks = [(0, 256, (0,)), (256, 256, (3,)), (512, 256, (4, 5)), (768, 128, (6,)), (896, 128, (1, 7))]
-        h_bf = [sb("h_bf%d" % c, [P, width, PACK], BF16, "slot_h%d" % c) for c, (c0, width, use) in enumerate(chunks)]
-        res_slot = ["slot_h1", "slot_h2", "res2", "res3", "res4"]
-        h_codes = shifted("h_codes", S, U32, 32)
-        h_scales = shifted("h_scales", S, U8, 192)
-
         def silu(b):
-            c = max(i for i, chunk in enumerate(chunks) if chunk[0] <= BANK * b)
-            n0 = BANK * b - chunks[c][0]
+            c = max(i for i, chunk in enumerate(CHUNKS) if chunk[0] <= BANK_TOKENS * b)
+            n0 = BANK_TOKENS * b - CHUNKS[c][0]
             nc.scalar.activation(
-                h_bf[c][:, n0 : n0 + BANK, :], banks[b][:].rearrange("p (t n) -> p n t", t=PACK), SILU
+                h_bf[c][:, n0 : n0 + BANK_TOKENS, :], hidden[b][:].rearrange("p (t n) -> p n t", t=PACK), SILU
             )
 
         quantize_w1(0)
-        nc.vector.tensor_copy(xs[0][ROW0:, :].bitcast(I32), xs_picked[ROW0:, :].bitcast(I32))
-        x_codes.append(shifted("x_codes0", S, U32, 32))
-        for c in range(S // GATHER):
-            gather(0, c)
-            first(0, 2 * c)
-            first(0, 2 * c + 1)
-        cast_w1(1)
+        nc.vector.tensor_copy(xs[0][TABLE_ROW0:, :].bitcast(I32), xs_picked[TABLE_ROW0:, :].bitcast(I32))
+        x_codes.append(words_at("x_codes0", S, LEAD_MOVING_CODES))
+        for i in range(S // GATHER):
+            gather_words(0, i)
+            for b in range(GATHER // BANK_TOKENS * i, GATHER // BANK_TOKENS * (i + 1)):
+                hidden_pass(0, b)
+        round_w1(1)
         quantize_w1(1)
-        x_codes.append(shifted("x_codes1", S, U32, 32))
-        for c in range(S // GATHER):
-            gather(1, c)
-            for b in (2 * c, 2 * c + 1):
-                first(1, b)
-                silu(b)
+        x_codes.append(words_at("x_codes1", S, LEAD_MOVING_CODES))
 
-        for c, (c0, width, use) in enumerate(chunks):
-            cols = slice(c0, c0 + width)
+        out_halves = out.rearrange("(m p) n -> p m n", p=P)
+        sums = {}
+
+        def h_cols(c):
+            return slice(H_COL0[c], H_COL0[c] + CHUNKS[c][1])
+
+        def quantize_h(c):
             nc.vector.quantize_mx(
-                out=h_codes[:, cols].bitcast(FP8X4),
-                scales=h_scales[:, cols],
+                out=h_codes[:, h_cols(c)].bitcast(FP8X4),
+                scales=h_scales[:, h_cols(c)],
                 in_=h_bf[c][:].rearrange("p n t -> p (n t)"),
             )
 
-        out_v = out.rearrange("(m p) n -> p m n", p=P)
-        for c, (c0, width, use) in enumerate(chunks):
-            cols = slice(c0, c0 + width)
-            tiles = [psum.tile([P, 512], F32, name="o%d_%d" % (c, b), tag="bank%d" % b) for b in use]
-            split = len(use) == 2
-            acc = [tiles[m][:, :width] if split else tiles[0][:, width * m : width * (m + 1)] for m in range(2)]
-            res = sb("res%d" % c, [P, 2, width], F32, res_slot[c])
-            for m in range(2):
-                mc = slice(P * m, P * (m + 1))
+        def shortcut(c):
+            tok0, width, banks = CHUNKS[c]
+            tokens = slice(tok0, tok0 + width)
+            tiles = [psum.tile([P, BANK_COLS], F32, name="o%d_%d" % (c, b), tag="bank%d" % b) for b in banks]
+            if len(banks) == HALVES:
+                sums[c] = [tile[:, :width] for tile in tiles]
+            else:
+                sums[c] = [tiles[0][:, width * m : width * (m + 1)] for m in range(HALVES)]
+                sums[c].append(tiles[0][:, : HALVES * width].rearrange("p (m n) -> p m n", m=HALVES))
+            for m in range(HALVES):
+                rows = slice(P * m, P * (m + 1))
                 for g in range(PASSES):
                     nc.tensor.matmul_mx(
-                        out=acc[m],
-                        lhsT=w23[:, g, mc].bitcast(FP8X4),
-                        lhsT_scale=ws[4 * g : P, mc],
-                        rhs=x_codes[g][:, cols].bitcast(FP8X4),
-                        rhs_scale=xs[g][PLANE[g] : P, cols],
-                        start=(g == 0 and (split or m == 0)),
+                        out=sums[c][m],
+                        lhsT=w23[:, g, rows].bitcast(FP8X4),
+                        lhsT_scale=ws[QUAD_ROWS * g : P, rows],
+                        rhs=x_codes[g][:, tokens].bitcast(FP8X4),
+                        rhs_scale=xs[g][X_PLANE[g] : P, tokens],
+                        start=(g == 0 and m < len(banks)),
                         stop=False,
                     )
-            for m in range(2):
-                mc = slice(P * m, P * (m + 1))
+
+        def close(c):
+            tok0, width, banks = CHUNKS[c]
+            result = sb("result%d" % c, [P, HALVES, width], F32)
+            for m in range(HALVES):
                 nc.tensor.matmul_mx(
-                    out=acc[m],
-                    lhsT=w23[:, PASSES, mc].bitcast(FP8X4),
-                    lhsT_scale=ws[8:P, mc],
-                    rhs=h_codes[:, cols].bitcast(FP8X4),
-                    rhs_scale=h_scales[:, cols],
+                    out=sums[c][m],
+                    lhsT=w23[:, PASSES, P * m : P * (m + 1)].bitcast(FP8X4),
+                    lhsT_scale=ws[:, N + P * m : N + P * (m + 1)],
+                    rhs=h_codes[:, h_cols(c)].bitcast(FP8X4),
+                    rhs_scale=h_scales[:, h_cols(c)],
                     start=False,
-                    stop=(split or m == 1),
+                    stop=(m >= HALVES - len(banks)),
                 )
-            if split:
-                nc.vector.tensor_copy(res[:, 0, :], acc[0])
-                nc.scalar.copy(res[:, 1, :], acc[1])
-                nc.sync.dma_start(out_v[:, :, cols], res[:])
-            else:
-                both = tiles[0][:, : 2 * width].rearrange("p (m n) -> p m n", m=2)
-                if c == len(chunks) - 2:
-                    nc.scalar.copy(res[:], both)
-                else:
-                    nc.vector.tensor_copy(res[:], both)
-                nc.sync.dma_start(out_v[:, :, cols], res[:])
+            return result, out_halves[:, :, tok0 : tok0 + width]
+
+        def store_whole(c, copy):
+            result, target = close(c)
+            copy(result[:], sums[c][HALVES])
+            nc.sync.dma_start(target, result[:])
+
+        for i in range(S // GATHER):
+            gather_words(1, i)
+        for b in range(BANKS):
+            if b == BANKS_BEFORE_SHORTCUT:
+                shortcut(0)
+            hidden_pass(1, b)
+            silu(b)
+
+        quantize_h(0)
+        quantize_h(1)
+        store_whole(0, nc.vector.tensor_copy)
+        quantize_h(2)
+        shortcut(1)
+        store_whole(1, nc.vector.tensor_copy)
+        quantize_h(3)
+        quantize_h(4)
+
+        shortcut(2)
+        result, target = close(2)
+        for m, copy in enumerate((nc.scalar.copy, nc.vector.tensor_copy)):
+            copy(result[:, m, :], sums[2][m])
+            nc.sync.dma_start(target[:, m, :], result[:, m, :])
+
+        shortcut(3)
+        store_whole(3, nc.scalar.copy)
+
+        shortcut(4)
+        result, target = close(4)
+        for m, copy in enumerate((nc.vector.tensor_copy, nc.scalar.copy)):
+            copy(result[:, m, :], sums[4][m])
+        nc.sync.dma_start(target, result[:])

@@ -26,18 +26,16 @@ LIST_ROWS = 16
 BANKS = 8
 BANK_COLS = 512
 BANK_TOKENS = S // BANKS
-GATHER = 256
 HALVES = N // P
 
 VECTOR_SHARE = (76, 80)
 W1_LEAD = 640
 TABLE_ROW0 = P - QUAD
 X_PLANE = (12, 4)
+GATHERS = ((256, 256, 256, 256), (128, 128, 128, 128, 128, 128, 256))
 BANKS_BEFORE_SHORTCUT = 6
 LEAD_STATIONARY_SCALES, LEAD_MOVING_CODES, LEAD_MOVING_SCALES = 64, 128, 192
-
-CHUNKS = ((0, 256, (0,)), (256, 256, (3,)), (512, 256, (4, 5)), (768, 128, (6,)), (896, 128, (1, 7)))
-H_COL0 = (0, 256, 512, 256, 896)
+CHUNKS = ((0, 256, (0,)), (256, 256, (1, 2)), (512, 256, (3, 4)), (768, 128, (5,)), (896, 128, (0, 6)))
 
 
 def tile_picked_zskip_silu_p_kernel(
@@ -63,7 +61,16 @@ def tile_picked_zskip_silu_p_kernel(
         xs_planes = bytes_at("xs_planes", PASSES * S, LEAD_MOVING_SCALES)
         xs = [xs_planes[:, S * g : S * (g + 1)] for g in range(PASSES)]
         ws = bytes_at("ws", 2 * N, LEAD_STATIONARY_SCALES)
-        w1_raw = sb("w1_raw", [P, PASSES * PACK * H], F32)
+        w1_raw = [sb("w1_raw%d" % g, [P, PACK, H], F32) for g in range(PASSES)]
+        w1_bf = [sb("w1_bf%d" % g, [P, PACK, P, PACK], BF16) for g in range(PASSES)]
+        w1_codes = [sb("w1_codes%d" % g, [P, H], U32) for g in range(PASSES)]
+        w1_scales = [bytes_at("w1_scales%d" % g, H, LEAD_STATIONARY_SCALES) for g in range(PASSES)]
+        x_table = [sb("x_table%d" % g, [P, T], I32) for g in range(PASSES)]
+        x_codes = [words_at("x_codes%d" % g, S, LEAD_MOVING_CODES) for g in range(PASSES)]
+        w23 = sb("w23", [P, PASSES + 1, N], I32)
+        h_bf = [sb("h_bf%d" % c, [P, width, PACK], BF16) for c, (tok0, width, banks) in enumerate(CHUNKS)]
+        h_codes = words_at("h_codes", S, LEAD_MOVING_CODES)
+        h_scales = bytes_at("h_scales", S, LEAD_MOVING_SCALES)
 
         warm = sb("warm", [P, 16], F32)
         warm_out = sb("warm_out", [P, 16], F32)
@@ -74,46 +81,42 @@ def tile_picked_zskip_silu_p_kernel(
         nc.vector.memset(xs_planes[:].bitcast(I32), 0)
         nc.gpsimd.memset(ws[:].bitcast(I32), 0)
 
-        w1_bf = [sb("w1_bf%d" % g, [P, PACK, P, PACK], BF16) for g in range(PASSES)]
-        w1_codes = [sb("w1_codes%d" % g, [P, H], U32) for g in range(PASSES)]
-        w1_scales = [bytes_at("w1_scales%d" % g, H, LEAD_STATIONARY_SCALES) for g in range(PASSES)]
-        w1_rows = w1_raw[:].rearrange("p (g j c) -> p g j c", g=PASSES, j=PACK)
-
         def load_w1(g, v0, v1):
             rows = w1[PASS_K * g : PASS_K * (g + 1), :].rearrange("(p j) c -> p (j c)", j=PACK)
-            nc.sync.dma_start(w1_raw[:, PACK * H * g + v0 : PACK * H * g + v1], rows[:, v0:v1])
+            nc.sync.dma_start(w1_raw[g][:].rearrange("p j c -> p (j c)")[:, v0:v1], rows[:, v0:v1])
 
-        def round_w1(g):
+        def load_x(g):
+            nc.sync.dma_start(x_table[g][:], x_words[g].rearrange("p n t -> p (n t)").bitcast(I32))
+
+        def move_scales(g, q):
+            src = TABLE_ROW0 + PLANE_ROWS * g + QUAD_ROWS * q
+            dst = QUAD * q + X_PLANE[g]
+            nc.sync.dma_start(
+                xs[g][dst : dst + QUAD_ROWS, :].bitcast(I32), xs_picked[src : src + QUAD_ROWS, :].bitcast(I32)
+            )
+
+        def prepare_w1(g):
             dst = w1_bf[g][:].rearrange("p t m j -> p m j t")
-            src = w1_rows[:, g].rearrange("p j (m t) -> p m j t", t=PACK)
+            src = w1_raw[g][:].rearrange("p j (m t) -> p m j t", t=PACK)
             nc.scalar.copy(dst[:, VECTOR_SHARE[g] :], src[:, VECTOR_SHARE[g] :])
             nc.vector.tensor_copy(dst[:, : VECTOR_SHARE[g]], src[:, : VECTOR_SHARE[g]])
-
-        def quantize_w1(g):
             nc.vector.quantize_mx(
                 out=w1_codes[g][:].bitcast(FP8X4),
                 scales=w1_scales[g][:],
                 in_=w1_bf[g][:].rearrange("p t m j -> p (t m j)"),
             )
 
-        def load_x(g):
-            table = sb("x_table%d" % g, [P, T], I32)
-            nc.sync.dma_start(table[:], x_words[g].rearrange("p n t -> p (n t)").bitcast(I32))
-            return table
-
-        def move_scales(g):
-            for q in (0, 2, 1, 3):
-                src = TABLE_ROW0 + PLANE_ROWS * g + QUAD_ROWS * q
-                dst = QUAD * q + X_PLANE[g]
-                if src != dst:
-                    nc.sync.dma_start(
-                        xs[g][dst : dst + QUAD_ROWS, :].bitcast(I32), xs_picked[src : src + QUAD_ROWS, :].bitcast(I32)
-                    )
+        def gather_words(g):
+            tok0 = 0
+            for width in GATHERS[g]:
+                entries = offsets[:, tok0 // LIST_ROWS : (tok0 + width) // LIST_ROWS]
+                nc.vector.tensor_copy(x_codes[g][:, tok0 : tok0 + width], x_table[g][:].bitcast(U32).indirect(entries))
+                tok0 = tok0 + width
 
         nc.sync.dma_start(offsets[:], offs)
         nc.sync.dma_start(xs_table[TABLE_ROW0:, :].bitcast(I32), x_scales.rearrange("g q n -> (g q) n").bitcast(I32))
         load_w1(0, 0, PACK * H)
-        x_table = [load_x(0)]
+        load_x(0)
         for q in range(QUADS):
             rows = slice(QUAD_ROWS * q, QUAD_ROWS * (q + 1))
             nc.gpsimd.dma_start(
@@ -124,26 +127,19 @@ def tile_picked_zskip_silu_p_kernel(
             nc.gpsimd.dma_start(ws[QUAD * q : QUAD * q + QUAD_ROWS, N:].bitcast(I32), w2_scales[0, rows, :].bitcast(I32))
         nc.vector.tensor_copy(xs_picked[:], xs_table[:].indirect(offsets[:]))
         load_w1(1, 0, W1_LEAD)
-        move_scales(0)
+        for q in (0, 2, 1):
+            move_scales(0, q)
         load_w1(1, W1_LEAD, PACK * H)
-        x_table.append(load_x(1))
-        move_scales(1)
-        w23 = sb("w23", [P, PASSES + 1, N], I32)
+        load_x(1)
+        for q in (0, 2, 1, 3):
+            move_scales(1, q)
         nc.sync.dma_start(w23[:, :PASSES, :], w3_words.rearrange("g p n t -> p g (n t)").bitcast(I32))
         nc.sync.dma_start(w23[:, PASSES, :], w2_words[0].rearrange("p n t -> p (n t)").bitcast(I32))
 
-        round_w1(0)
-        hidden = [psum.tile([P, BANK_COLS], F32, name="h%d" % b, tag="bank%d" % b) for b in range(BANKS)]
-        h_bf = [sb("h_bf%d" % c, [P, width, PACK], BF16) for c, (tok0, width, banks) in enumerate(CHUNKS)]
-        h_codes = words_at("h_codes", S, LEAD_MOVING_CODES)
-        h_scales = bytes_at("h_scales", S, LEAD_MOVING_SCALES)
-        x_codes = []
+        prepare_w1(0)
+        nc.vector.tensor_copy(xs[0][TABLE_ROW0:, :].bitcast(I32), xs_picked[TABLE_ROW0:, :].bitcast(I32))
 
-        def gather_words(g, i):
-            entries = offsets[:, GATHER // LIST_ROWS * i : GATHER // LIST_ROWS * (i + 1)]
-            nc.vector.tensor_copy(
-                x_codes[g][:, GATHER * i : GATHER * (i + 1)], x_table[g][:].bitcast(U32).indirect(entries)
-            )
+        hidden = [psum.tile([P, BANK_COLS], F32, name="h%d" % b, tag="bank%d" % b) for b in range(BANKS)]
 
         def hidden_pass(g, b):
             tokens = slice(BANK_TOKENS * b, BANK_TOKENS * (b + 1))
@@ -166,33 +162,27 @@ def tile_picked_zskip_silu_p_kernel(
                 h_bf[c][:, n0 : n0 + BANK_TOKENS, :], hidden[b][:].rearrange("p (t n) -> p n t", t=PACK), SILU
             )
 
-        quantize_w1(0)
-        nc.vector.tensor_copy(xs[0][TABLE_ROW0:, :].bitcast(I32), xs_picked[TABLE_ROW0:, :].bitcast(I32))
-        x_codes.append(words_at("x_codes0", S, LEAD_MOVING_CODES))
-        for i in range(S // GATHER):
-            gather_words(0, i)
-            for b in range(GATHER // BANK_TOKENS * i, GATHER // BANK_TOKENS * (i + 1)):
-                hidden_pass(0, b)
-        round_w1(1)
-        quantize_w1(1)
-        x_codes.append(words_at("x_codes1", S, LEAD_MOVING_CODES))
+        gather_words(0)
+        for b in range(BANKS):
+            hidden_pass(0, b)
+        prepare_w1(1)
 
         out_halves = out.rearrange("(m p) n -> p m n", p=P)
         sums = {}
+        result = [sb("result%d" % c, [P, HALVES, width], F32) for c, (tok0, width, banks) in enumerate(CHUNKS)]
 
-        def h_cols(c):
-            return slice(H_COL0[c], H_COL0[c] + CHUNKS[c][1])
+        def tokens_of(c):
+            return slice(CHUNKS[c][0], CHUNKS[c][0] + CHUNKS[c][1])
 
         def quantize_h(c):
             nc.vector.quantize_mx(
-                out=h_codes[:, h_cols(c)].bitcast(FP8X4),
-                scales=h_scales[:, h_cols(c)],
+                out=h_codes[:, tokens_of(c)].bitcast(FP8X4),
+                scales=h_scales[:, tokens_of(c)],
                 in_=h_bf[c][:].rearrange("p n t -> p (n t)"),
             )
 
         def shortcut(c):
             tok0, width, banks = CHUNKS[c]
-            tokens = slice(tok0, tok0 + width)
             tiles = [psum.tile([P, BANK_COLS], F32, name="o%d_%d" % (c, b), tag="bank%d" % b) for b in banks]
             if len(banks) == HALVES:
                 sums[c] = [tile[:, :width] for tile in tiles]
@@ -206,60 +196,62 @@ def tile_picked_zskip_silu_p_kernel(
                         out=sums[c][m],
                         lhsT=w23[:, g, rows].bitcast(FP8X4),
                         lhsT_scale=ws[QUAD_ROWS * g : P, rows],
-                        rhs=x_codes[g][:, tokens].bitcast(FP8X4),
-                        rhs_scale=xs[g][X_PLANE[g] : P, tokens],
+                        rhs=x_codes[g][:, tokens_of(c)].bitcast(FP8X4),
+                        rhs_scale=xs[g][X_PLANE[g] : P, tokens_of(c)],
                         start=(g == 0 and m < len(banks)),
                         stop=False,
                     )
 
         def close(c):
-            tok0, width, banks = CHUNKS[c]
-            result = sb("result%d" % c, [P, HALVES, width], F32)
+            banks = CHUNKS[c][2]
             for m in range(HALVES):
                 nc.tensor.matmul_mx(
                     out=sums[c][m],
                     lhsT=w23[:, PASSES, P * m : P * (m + 1)].bitcast(FP8X4),
                     lhsT_scale=ws[:, N + P * m : N + P * (m + 1)],
-                    rhs=h_codes[:, h_cols(c)].bitcast(FP8X4),
-                    rhs_scale=h_scales[:, h_cols(c)],
+                    rhs=h_codes[:, tokens_of(c)].bitcast(FP8X4),
+                    rhs_scale=h_scales[:, tokens_of(c)],
                     start=False,
                     stop=(m >= HALVES - len(banks)),
                 )
-            return result, out_halves[:, :, tok0 : tok0 + width]
 
         def store_whole(c, copy):
-            result, target = close(c)
-            copy(result[:], sums[c][HALVES])
-            nc.sync.dma_start(target, result[:])
+            copy(result[c][:], sums[c][HALVES])
+            nc.sync.dma_start(out_halves[:, :, tokens_of(c)], result[c][:])
 
-        for i in range(S // GATHER):
-            gather_words(1, i)
-        for b in range(BANKS):
-            if b == BANKS_BEFORE_SHORTCUT:
-                shortcut(0)
+        def store_half(c, m, copy):
+            copy(result[c][:, m, :], sums[c][m])
+            nc.sync.dma_start(out_halves[:, m, tokens_of(c)], result[c][:, m, :])
+
+        gather_words(1)
+        for b in range(BANKS_BEFORE_SHORTCUT):
             hidden_pass(1, b)
             silu(b)
-
         quantize_h(0)
+        shortcut(0)
+        close(0)
+        hidden_pass(1, 6)
+        silu(6)
         quantize_h(1)
         store_whole(0, nc.vector.tensor_copy)
-        quantize_h(2)
         shortcut(1)
-        store_whole(1, nc.vector.tensor_copy)
+        hidden_pass(1, 7)
+        silu(7)
+        close(1)
+        quantize_h(2)
+        for m in range(HALVES):
+            store_half(1, m, nc.vector.tensor_copy)
         quantize_h(3)
-        quantize_h(4)
-
         shortcut(2)
-        result, target = close(2)
-        for m, copy in enumerate((nc.scalar.copy, nc.vector.tensor_copy)):
-            copy(result[:, m, :], sums[2][m])
-            nc.sync.dma_start(target[:, m, :], result[:, m, :])
-
+        close(2)
+        store_half(2, 0, nc.scalar.copy)
+        quantize_h(4)
+        store_half(2, 1, nc.vector.tensor_copy)
         shortcut(3)
+        close(3)
         store_whole(3, nc.scalar.copy)
-
         shortcut(4)
-        result, target = close(4)
+        close(4)
         for m, copy in enumerate((nc.vector.tensor_copy, nc.scalar.copy)):
-            copy(result[:, m, :], sums[4][m])
-        nc.sync.dma_start(target, result[:])
+            copy(result[4][:, m, :], sums[4][m])
+        nc.sync.dma_start(out_halves[:, :, tokens_of(4)], result[4][:])

@@ -88,12 +88,13 @@ def tile_picked_zskip_silu_p_kernel(
         def load_x(g):
             nc.sync.dma_start(x_table[g][:], x_words[g].rearrange("p n t -> p (n t)").bitcast(I32))
 
-        def move_scales(g, q):
-            src = TABLE_ROW0 + PLANE_ROWS * g + QUAD_ROWS * q
-            dst = QUAD * q + X_PLANE[g]
-            nc.sync.dma_start(
-                xs[g][dst : dst + QUAD_ROWS, :].bitcast(I32), xs_picked[src : src + QUAD_ROWS, :].bitcast(I32)
-            )
+        def move_scales(g):
+            for r in range(QUAD_ROWS):
+                src = TABLE_ROW0 + PLANE_ROWS * g + r
+                nc.sync.dma_start(
+                    xs[g][X_PLANE[g] + r : P : QUAD, :].bitcast(I32),
+                    xs_picked[src : src - r + PLANE_ROWS : QUAD_ROWS, :].bitcast(I32),
+                )
 
         def prepare_w1(g):
             dst = w1_bf[g][:].rearrange("p t m j -> p m j t")
@@ -127,17 +128,14 @@ def tile_picked_zskip_silu_p_kernel(
             nc.gpsimd.dma_start(ws[QUAD * q : QUAD * q + QUAD_ROWS, N:].bitcast(I32), w2_scales[0, rows, :].bitcast(I32))
         nc.vector.tensor_copy(xs_picked[:], xs_table[:].indirect(offsets[:]))
         load_w1(1, 0, W1_LEAD)
-        for q in (0, 2, 1):
-            move_scales(0, q)
+        move_scales(0)
         load_w1(1, W1_LEAD, PACK * H)
         load_x(1)
-        for q in (0, 2, 1, 3):
-            move_scales(1, q)
+        move_scales(1)
         nc.sync.dma_start(w23[:, :PASSES, :], w3_words.rearrange("g p n t -> p g (n t)").bitcast(I32))
         nc.sync.dma_start(w23[:, PASSES, :], w2_words[0].rearrange("p n t -> p (n t)").bitcast(I32))
 
         prepare_w1(0)
-        nc.vector.tensor_copy(xs[0][TABLE_ROW0:, :].bitcast(I32), xs_picked[TABLE_ROW0:, :].bitcast(I32))
 
         hidden = [psum.tile([P, BANK_COLS], F32, name="h%d" % b, tag="bank%d" % b) for b in range(BANKS)]
 

@@ -32,10 +32,10 @@ VECTOR_SHARE = (76, 80)
 W1_LEAD = 640
 TABLE_ROW0 = P - QUAD
 X_PLANE = (12, 4)
-GATHERS = ((256, 256, 256, 256), (128, 128, 128, 128, 128, 128, 256))
-BANKS_BEFORE_SHORTCUT = 6
-LEAD_STATIONARY_SCALES, LEAD_MOVING_CODES, LEAD_MOVING_SCALES = 64, 128, 192
+GATHERS = ((256, 256, 256, 256), (128, 128, 128, 128, 128, 128, 128, 128))
+LEAD_STATIONARY_CODES, LEAD_STATIONARY_SCALES, LEAD_MOVING_CODES, LEAD_MOVING_SCALES = 64, 0, 128, 192
 CHUNKS = ((0, 256, (0,)), (256, 256, (1, 2)), (512, 256, (3, 4)), (768, 128, (5,)), (896, 128, (0, 6)))
+H_COL0 = (0, 256, 0, 256, 384)
 
 
 def tile_picked_zskip_silu_p_kernel(
@@ -60,14 +60,15 @@ def tile_picked_zskip_silu_p_kernel(
         xs_picked = sb("xs_picked", [P, S], U8)
         xs_planes = bytes_at("xs_planes", PASSES * S, LEAD_MOVING_SCALES)
         xs = [xs_planes[:, S * g : S * (g + 1)] for g in range(PASSES)]
-        ws = bytes_at("ws", 2 * N, LEAD_STATIONARY_SCALES)
+        ws = bytes_at("ws", (PASSES + 1) * N, LEAD_STATIONARY_SCALES)
         w1_raw = [sb("w1_raw%d" % g, [P, PACK, H], F32) for g in range(PASSES)]
         w1_bf = [sb("w1_bf%d" % g, [P, PACK, P, PACK], BF16) for g in range(PASSES)]
-        w1_codes = [sb("w1_codes%d" % g, [P, H], U32) for g in range(PASSES)]
+        w1_codes = [words_at("w1_codes%d" % g, H, LEAD_STATIONARY_CODES) for g in range(PASSES)]
         w1_scales = [bytes_at("w1_scales%d" % g, H, LEAD_STATIONARY_SCALES) for g in range(PASSES)]
         x_table = [sb("x_table%d" % g, [P, T], I32) for g in range(PASSES)]
         x_codes = [words_at("x_codes%d" % g, S, LEAD_MOVING_CODES) for g in range(PASSES)]
-        w23 = sb("w23", [P, PASSES + 1, N], I32)
+        w23_row = sb("w23", [P, LEAD_STATIONARY_CODES // PACK + (PASSES + 1) * N], I32)[:, LEAD_STATIONARY_CODES // PACK :]
+        w23 = w23_row.rearrange("p (g n) -> p g n", n=N)
         h_bf = [sb("h_bf%d" % c, [P, width, PACK], BF16) for c, (tok0, width, banks) in enumerate(CHUNKS)]
         h_codes = words_at("h_codes", S, LEAD_MOVING_CODES)
         h_scales = bytes_at("h_scales", S, LEAD_MOVING_SCALES)
@@ -79,7 +80,7 @@ def tile_picked_zskip_silu_p_kernel(
 
         nc.vector.memset(xs_table[:TABLE_ROW0, :].bitcast(I32), 0)
         nc.vector.memset(xs_planes[:].bitcast(I32), 0)
-        nc.gpsimd.memset(ws[:].bitcast(I32), 0)
+        nc.vector.memset(ws.bitcast(I32), 0)
 
         def load_w1(g, v0, v1):
             rows = w1[PASS_K * g : PASS_K * (g + 1), :].rearrange("(p j) c -> p (j c)", j=PACK)
@@ -102,8 +103,8 @@ def tile_picked_zskip_silu_p_kernel(
             nc.scalar.copy(dst[:, VECTOR_SHARE[g] :], src[:, VECTOR_SHARE[g] :])
             nc.vector.tensor_copy(dst[:, : VECTOR_SHARE[g]], src[:, : VECTOR_SHARE[g]])
             nc.vector.quantize_mx(
-                out=w1_codes[g][:].bitcast(FP8X4),
-                scales=w1_scales[g][:],
+                out=w1_codes[g].bitcast(FP8X4),
+                scales=w1_scales[g],
                 in_=w1_bf[g][:].rearrange("p t m j -> p (t m j)"),
             )
 
@@ -118,14 +119,6 @@ def tile_picked_zskip_silu_p_kernel(
         nc.sync.dma_start(xs_table[TABLE_ROW0:, :].bitcast(I32), x_scales.rearrange("g q n -> (g q) n").bitcast(I32))
         load_w1(0, 0, PACK * H)
         load_x(0)
-        for q in range(QUADS):
-            rows = slice(QUAD_ROWS * q, QUAD_ROWS * (q + 1))
-            nc.gpsimd.dma_start(
-                ws[QUAD * q : QUAD * q + PASSES * QUAD_ROWS, :N].bitcast(I32), w3_scales[:, rows, :].bitcast(I32)
-            )
-        for q in range(QUADS):
-            rows = slice(QUAD_ROWS * q, QUAD_ROWS * (q + 1))
-            nc.gpsimd.dma_start(ws[QUAD * q : QUAD * q + QUAD_ROWS, N:].bitcast(I32), w2_scales[0, rows, :].bitcast(I32))
         nc.vector.tensor_copy(xs_picked[:], xs_table[:].indirect(offsets[:]))
         load_w1(1, 0, W1_LEAD)
         move_scales(0)
@@ -134,6 +127,13 @@ def tile_picked_zskip_silu_p_kernel(
         move_scales(1)
         nc.sync.dma_start(w23[:, :PASSES, :], w3_words.rearrange("g p n t -> p g (n t)").bitcast(I32))
         nc.sync.dma_start(w23[:, PASSES, :], w2_words[0].rearrange("p n t -> p (n t)").bitcast(I32))
+        for r in range(QUAD_ROWS):
+            nc.sync.dma_start(ws[r:P:QUAD, PASSES * N :].bitcast(I32), w2_scales[0, r::QUAD_ROWS, :].bitcast(I32))
+        for r in range(QUAD_ROWS):
+            nc.sync.dma_start(
+                ws[r:P:QUAD, : PASSES * N].bitcast(I32).rearrange("q (g n) -> q g n", g=PASSES),
+                w3_scales[:, r::QUAD_ROWS, :].bitcast(I32).rearrange("g q n -> q g n"),
+            )
 
         prepare_w1(0)
 
@@ -172,10 +172,13 @@ def tile_picked_zskip_silu_p_kernel(
         def tokens_of(c):
             return slice(CHUNKS[c][0], CHUNKS[c][0] + CHUNKS[c][1])
 
+        def h_cols(c):
+            return slice(H_COL0[c], H_COL0[c] + CHUNKS[c][1])
+
         def quantize_h(c):
             nc.vector.quantize_mx(
-                out=h_codes[:, tokens_of(c)].bitcast(FP8X4),
-                scales=h_scales[:, tokens_of(c)],
+                out=h_codes[:, h_cols(c)].bitcast(FP8X4),
+                scales=h_scales[:, h_cols(c)],
                 in_=h_bf[c][:].rearrange("p n t -> p (n t)"),
             )
 
@@ -193,7 +196,7 @@ def tile_picked_zskip_silu_p_kernel(
                     nc.tensor.matmul_mx(
                         out=sums[c][m],
                         lhsT=w23[:, g, rows].bitcast(FP8X4),
-                        lhsT_scale=ws[QUAD_ROWS * g : P, rows],
+                        lhsT_scale=ws[:, N * g + P * m : N * g + P * (m + 1)],
                         rhs=x_codes[g][:, tokens_of(c)].bitcast(FP8X4),
                         rhs_scale=xs[g][X_PLANE[g] : P, tokens_of(c)],
                         start=(g == 0 and m < len(banks)),
@@ -206,9 +209,9 @@ def tile_picked_zskip_silu_p_kernel(
                 nc.tensor.matmul_mx(
                     out=sums[c][m],
                     lhsT=w23[:, PASSES, P * m : P * (m + 1)].bitcast(FP8X4),
-                    lhsT_scale=ws[:, N + P * m : N + P * (m + 1)],
-                    rhs=h_codes[:, tokens_of(c)].bitcast(FP8X4),
-                    rhs_scale=h_scales[:, tokens_of(c)],
+                    lhsT_scale=ws[:, PASSES * N + P * m : PASSES * N + P * (m + 1)],
+                    rhs=h_codes[:, h_cols(c)].bitcast(FP8X4),
+                    rhs_scale=h_scales[:, h_cols(c)],
                     start=False,
                     stop=(m >= HALVES - len(banks)),
                 )
@@ -222,21 +225,17 @@ def tile_picked_zskip_silu_p_kernel(
             nc.sync.dma_start(out_halves[:, m, tokens_of(c)], result[c][:, m, :])
 
         gather_words(1)
-        for b in range(BANKS_BEFORE_SHORTCUT):
+        for b in range(BANKS):
             hidden_pass(1, b)
             silu(b)
         quantize_h(0)
+        quantize_h(1)
         shortcut(0)
         close(0)
-        hidden_pass(1, 6)
-        silu(6)
-        quantize_h(1)
         store_whole(0, nc.vector.tensor_copy)
-        shortcut(1)
-        hidden_pass(1, 7)
-        silu(7)
-        close(1)
         quantize_h(2)
+        shortcut(1)
+        close(1)
         for m in range(HALVES):
             store_half(1, m, nc.vector.tensor_copy)
         quantize_h(3)

@@ -126,9 +126,9 @@ def tile_picked_zskip_silu_p_kernel(
         load_x(1)
         move_scales(1)
         nc.sync.dma_start(w23[:, :PASSES, :], w3_words.rearrange("g p n t -> p g (n t)").bitcast(I32))
-        nc.sync.dma_start(w23[:, PASSES, :], w2_words[0].rearrange("p n t -> p (n t)").bitcast(I32))
         for r in range(QUAD_ROWS):
             nc.sync.dma_start(ws[r:P:QUAD, PASSES * N :].bitcast(I32), w2_scales[0, r::QUAD_ROWS, :].bitcast(I32))
+        nc.sync.dma_start(w23[:, PASSES, :], w2_words[0].rearrange("p n t -> p (n t)").bitcast(I32))
         for r in range(QUAD_ROWS):
             nc.sync.dma_start(
                 ws[r:P:QUAD, : PASSES * N].bitcast(I32).rearrange("q (g n) -> q g n", g=PASSES),

@@ -21,18 +21,19 @@ PASSES = K // PASS_K
 QUADS = 4
 QUAD = P // QUADS
 QUAD_ROWS = 4
-PLANE_ROWS = QUADS * QUAD_ROWS
 LIST_ROWS = 16
 BANKS = 8
 BANK_COLS = 512
 BANK_TOKENS = S // BANKS
 HALVES = N // P
 
-VECTOR_SHARE = (76, 80)
-W1_LEAD = 640
-TABLE_ROW0 = P - QUAD
-X_PLANE = (12, 4)
-GATHERS = ((256, 256, 256, 256), (128, 128, 128, 128, 128, 128, 128, 128))
+VECTOR_SHARE = (40, 64)
+W1_FIRST = (256, 1152)
+SPREAD_STEP = 4
+SPREAD_ROW0 = 1
+ROW_IN_PLACE = 1
+X_PLANE = (8, 12)
+GATHERS = ((128, 384, 512), (128, 128, 128, 128, 128, 128, 128, 128))
 LEAD_STATIONARY_CODES, LEAD_STATIONARY_SCALES, LEAD_MOVING_CODES, LEAD_MOVING_SCALES = 64, 0, 128, 192
 CHUNKS = ((0, 256, (0,)), (256, 256, (1, 2)), (512, 256, (3, 4)), (768, 128, (5,)), (896, 128, (0, 6)))
 H_COL0 = (0, 256, 0, 256, 384)
@@ -46,11 +47,11 @@ def tile_picked_zskip_silu_p_kernel(
         keep = ctx.enter_context(tc.tile_pool(name="keep", bufs=1))
         psum = ctx.enter_context(tc.psum_pool(name="psum", bufs=1))
 
-        def sb(name, shape, dtype):
-            return keep.tile(shape, dtype, name=name, align_bytes=256)
+        def sb(name, shape, dtype, tag=None):
+            return keep.tile(shape, dtype, name=name, tag=tag or name, align_bytes=256)
 
-        def bytes_at(name, width, lead):
-            return sb(name, [P, lead + width], U8)[:, lead:]
+        def bytes_at(name, width, lead, tag=None):
+            return sb(name, [P, lead + width], U8, tag)[:, lead:]
 
         def words_at(name, width, lead):
             return sb(name, [P, lead // PACK + width], U32)[:, lead // PACK :]
@@ -58,8 +59,7 @@ def tile_picked_zskip_silu_p_kernel(
         offsets = sb("offsets", [P, S // LIST_ROWS], U16)
         xs_table = sb("xs_table", [P, T], U8)
         xs_picked = sb("xs_picked", [P, S], U8)
-        xs_planes = bytes_at("xs_planes", PASSES * S, LEAD_MOVING_SCALES)
-        xs = [xs_planes[:, S * g : S * (g + 1)] for g in range(PASSES)]
+        xs = [bytes_at("xs0", S, LEAD_MOVING_SCALES)]
         ws = bytes_at("ws", (PASSES + 1) * N, LEAD_STATIONARY_SCALES)
         w1_raw = [sb("w1_raw%d" % g, [P, PACK, H], F32) for g in range(PASSES)]
         w1_bf = [sb("w1_bf%d" % g, [P, PACK, P, PACK], BF16) for g in range(PASSES)]
@@ -73,13 +73,13 @@ def tile_picked_zskip_silu_p_kernel(
         h_codes = words_at("h_codes", S, LEAD_MOVING_CODES)
         h_scales = bytes_at("h_scales", S, LEAD_MOVING_SCALES)
 
+        nc.vector.memset(xs_table[:].bitcast(I32), 0)
+
         warm = sb("warm", [P, 16], F32)
         warm_out = sb("warm_out", [P, 16], F32)
         nc.vector.memset(warm[:], 0.0)
         nc.scalar.activation(warm_out[:], warm[:], SILU)
 
-        nc.vector.memset(xs_table[:TABLE_ROW0, :].bitcast(I32), 0)
-        nc.vector.memset(xs_planes[:].bitcast(I32), 0)
         nc.vector.memset(ws.bitcast(I32), 0)
 
         def load_w1(g, v0, v1):
@@ -89,19 +89,24 @@ def tile_picked_zskip_silu_p_kernel(
         def load_x(g):
             nc.sync.dma_start(x_table[g][:], x_words[g].rearrange("p n t -> p (n t)").bitcast(I32))
 
+        def copy_scales(g):
+            nc.vector.tensor_copy(xs[g].bitcast(I32), xs_picked[:].bitcast(I32))
+
         def move_scales(g):
             for r in range(QUAD_ROWS):
-                src = TABLE_ROW0 + PLANE_ROWS * g + r
-                nc.sync.dma_start(
-                    xs[g][X_PLANE[g] + r : P : QUAD, :].bitcast(I32),
-                    xs_picked[src : src - r + PLANE_ROWS : QUAD_ROWS, :].bitcast(I32),
-                )
+                if r != ROW_IN_PLACE:
+                    src = SPREAD_ROW0 + SPREAD_STEP * (PASSES * r + g)
+                    nc.sync.dma_start(
+                        xs[g][X_PLANE[g] + r : P : QUAD, :].bitcast(I32), xs_picked[src:P:QUAD, :].bitcast(I32)
+                    )
 
-        def prepare_w1(g):
+        def round_w1(g):
             dst = w1_bf[g][:].rearrange("p t m j -> p m j t")
             src = w1_raw[g][:].rearrange("p j (m t) -> p m j t", t=PACK)
             nc.scalar.copy(dst[:, VECTOR_SHARE[g] :], src[:, VECTOR_SHARE[g] :])
             nc.vector.tensor_copy(dst[:, : VECTOR_SHARE[g]], src[:, : VECTOR_SHARE[g]])
+
+        def quantize_w1(g):
             nc.vector.quantize_mx(
                 out=w1_codes[g].bitcast(FP8X4),
                 scales=w1_scales[g],
@@ -115,27 +120,40 @@ def tile_picked_zskip_silu_p_kernel(
                 nc.vector.tensor_copy(x_codes[g][:, tok0 : tok0 + width], x_table[g][:].bitcast(U32).indirect(entries))
                 tok0 = tok0 + width
 
-        nc.sync.dma_start(offsets[:], offs)
-        nc.sync.dma_start(xs_table[TABLE_ROW0:, :].bitcast(I32), x_scales.rearrange("g q n -> (g q) n").bitcast(I32))
-        load_w1(0, 0, PACK * H)
-        load_x(0)
-        nc.vector.tensor_copy(xs_picked[:], xs_table[:].indirect(offsets[:]))
-        load_w1(1, 0, W1_LEAD)
-        move_scales(0)
-        load_w1(1, W1_LEAD, PACK * H)
-        load_x(1)
-        move_scales(1)
-        nc.sync.dma_start(w23[:, :PASSES, :], w3_words.rearrange("g p n t -> p g (n t)").bitcast(I32))
-        for r in range(QUAD_ROWS):
+        def load_w2_scales(r):
             nc.sync.dma_start(ws[r:P:QUAD, PASSES * N :].bitcast(I32), w2_scales[0, r::QUAD_ROWS, :].bitcast(I32))
-        nc.sync.dma_start(w23[:, PASSES, :], w2_words[0].rearrange("p n t -> p (n t)").bitcast(I32))
-        for r in range(QUAD_ROWS):
+
+        def load_w3_scales(r):
             nc.sync.dma_start(
                 ws[r:P:QUAD, : PASSES * N].bitcast(I32).rearrange("q (g n) -> q g n", g=PASSES),
                 w3_scales[:, r::QUAD_ROWS, :].bitcast(I32).rearrange("g q n -> q g n"),
             )
 
-        prepare_w1(0)
+        load_w1(0, 0, W1_FIRST[0])
+        nc.sync.dma_start(offsets[:], offs)
+        nc.sync.dma_start(
+            xs_table[SPREAD_ROW0:P:SPREAD_STEP, :].bitcast(I32), x_scales.rearrange("g q n -> q g n").bitcast(I32)
+        )
+        load_w1(0, W1_FIRST[0], PACK * H)
+        load_x(0)
+        nc.vector.tensor_copy(xs_picked[:], xs_table[:].indirect(offsets[:]))
+        copy_scales(0)
+        load_w1(1, 0, W1_FIRST[1])
+        move_scales(0)
+        load_w1(1, W1_FIRST[1], PACK * H)
+        load_x(1)
+        round_w1(0)
+        xs.append(bytes_at("xs1", S, LEAD_MOVING_SCALES, "w1_raw0"))
+        copy_scales(1)
+        quantize_w1(0)
+        move_scales(1)
+        for r in range(QUAD_ROWS - 1):
+            load_w2_scales(r)
+        nc.sync.dma_start(w23[:, :PASSES, :], w3_words.rearrange("g p n t -> p g (n t)").bitcast(I32))
+        load_w2_scales(QUAD_ROWS - 1)
+        nc.sync.dma_start(w23[:, PASSES, :], w2_words[0].rearrange("p n t -> p (n t)").bitcast(I32))
+        for r in range(QUAD_ROWS):
+            load_w3_scales(r)
 
         hidden = [psum.tile([P, BANK_COLS], F32, name="h%d" % b, tag="bank%d" % b) for b in range(BANKS)]
 
@@ -163,7 +181,8 @@ def tile_picked_zskip_silu_p_kernel(
         gather_words(0)
         for b in range(BANKS):
             hidden_pass(0, b)
-        prepare_w1(1)
+        round_w1(1)
+        quantize_w1(1)
 
         out_halves = out.rearrange("(m p) n -> p m n", p=P)
         sums = {}
@@ -175,14 +194,15 @@ def tile_picked_zskip_silu_p_kernel(
         def h_cols(c):
             return slice(H_COL0[c], H_COL0[c] + CHUNKS[c][1])
 
-        def quantize_h(c):
+        def quantize_h(c, n0, n1):
+            cols = slice(H_COL0[c] + n0, H_COL0[c] + n1)
             nc.vector.quantize_mx(
-                out=h_codes[:, h_cols(c)].bitcast(FP8X4),
-                scales=h_scales[:, h_cols(c)],
-                in_=h_bf[c][:].rearrange("p n t -> p (n t)"),
+                out=h_codes[:, cols].bitcast(FP8X4),
+                scales=h_scales[:, cols],
+                in_=h_bf[c][:, n0:n1, :].rearrange("p n t -> p (n t)"),
             )
 
-        def shortcut(c):
+        def open_sums(c):
             tok0, width, banks = CHUNKS[c]
             tiles = [psum.tile([P, BANK_COLS], F32, name="o%d_%d" % (c, b), tag="bank%d" % b) for b in banks]
             if len(banks) == HALVES:
@@ -190,31 +210,42 @@ def tile_picked_zskip_silu_p_kernel(
             else:
                 sums[c] = [tiles[0][:, width * m : width * (m + 1)] for m in range(HALVES)]
                 sums[c].append(tiles[0][:, : HALVES * width].rearrange("p (m n) -> p m n", m=HALVES))
-            for m in range(HALVES):
-                rows = slice(P * m, P * (m + 1))
-                for g in range(PASSES):
-                    nc.tensor.matmul_mx(
-                        out=sums[c][m],
-                        lhsT=w23[:, g, rows].bitcast(FP8X4),
-                        lhsT_scale=ws[:, N * g + P * m : N * g + P * (m + 1)],
-                        rhs=x_codes[g][:, tokens_of(c)].bitcast(FP8X4),
-                        rhs_scale=xs[g][X_PLANE[g] : P, tokens_of(c)],
-                        start=(g == 0 and m < len(banks)),
-                        stop=False,
-                    )
 
-        def close(c):
-            banks = CHUNKS[c][2]
-            for m in range(HALVES):
+        def shortcut(c, m):
+            for g in range(PASSES):
                 nc.tensor.matmul_mx(
                     out=sums[c][m],
-                    lhsT=w23[:, PASSES, P * m : P * (m + 1)].bitcast(FP8X4),
-                    lhsT_scale=ws[:, PASSES * N + P * m : PASSES * N + P * (m + 1)],
-                    rhs=h_codes[:, h_cols(c)].bitcast(FP8X4),
-                    rhs_scale=h_scales[:, h_cols(c)],
-                    start=False,
-                    stop=(m >= HALVES - len(banks)),
+                    lhsT=w23[:, g, P * m : P * (m + 1)].bitcast(FP8X4),
+                    lhsT_scale=ws[:, N * g + P * m : N * g + P * (m + 1)],
+                    rhs=x_codes[g][:, tokens_of(c)].bitcast(FP8X4),
+                    rhs_scale=xs[g][X_PLANE[g] : P, tokens_of(c)],
+                    start=(g == 0 and m < len(CHUNKS[c][2])),
+                    stop=False,
                 )
+
+        def close(c, m):
+            nc.tensor.matmul_mx(
+                out=sums[c][m],
+                lhsT=w23[:, PASSES, P * m : P * (m + 1)].bitcast(FP8X4),
+                lhsT_scale=ws[:, PASSES * N + P * m : PASSES * N + P * (m + 1)],
+                rhs=h_codes[:, h_cols(c)].bitcast(FP8X4),
+                rhs_scale=h_scales[:, h_cols(c)],
+                start=False,
+                stop=(m >= HALVES - len(CHUNKS[c][2])),
+            )
+
+        def products_half_by_half(c):
+            open_sums(c)
+            for m in range(HALVES):
+                shortcut(c, m)
+                close(c, m)
+
+        def products_shortcuts_first(c):
+            open_sums(c)
+            for m in range(HALVES):
+                shortcut(c, m)
+            for m in range(HALVES):
+                close(c, m)
 
         def store_whole(c, copy):
             copy(result[c][:], sums[c][HALVES])
@@ -228,27 +259,21 @@ def tile_picked_zskip_silu_p_kernel(
         for b in range(BANKS):
             hidden_pass(1, b)
             silu(b)
-        quantize_h(0)
-        quantize_h(1)
-        shortcut(0)
-        close(0)
+        quantize_h(0, 0, 256)
+        quantize_h(1, 0, 256)
+        products_shortcuts_first(0)
         store_whole(0, nc.vector.tensor_copy)
-        quantize_h(2)
-        shortcut(1)
-        close(1)
+        quantize_h(2, 0, 256)
+        products_shortcuts_first(1)
         for m in range(HALVES):
             store_half(1, m, nc.vector.tensor_copy)
-        quantize_h(3)
-        shortcut(2)
-        close(2)
+        quantize_h(3, 0, 128)
+        products_shortcuts_first(2)
         store_half(2, 0, nc.scalar.copy)
-        quantize_h(4)
+        quantize_h(4, 0, 128)
         store_half(2, 1, nc.vector.tensor_copy)
-        shortcut(3)
-        close(3)
+        products_shortcuts_first(3)
         store_whole(3, nc.scalar.copy)
-        shortcut(4)
-        close(4)
-        for m, copy in enumerate((nc.vector.tensor_copy, nc.scalar.copy)):
-            copy(result[4][:, m, :], sums[4][m])
-        nc.sync.dma_start(out_halves[:, :, tokens_of(4)], result[4][:])
+        products_half_by_half(4)
+        store_half(4, 0, nc.vector.tensor_copy)
+        store_half(4, 1, nc.scalar.copy)

@@ -27,8 +27,8 @@ BANK_COLS = 512
 BANK_TOKENS = S // BANKS
 HALVES = N // P
 
-VECTOR_SHARE = (40, 64)
-W1_FIRST = (256, 1152)
+VECTOR_SHARE = (44, 64)
+W1_FIRST = (384, 1408)
 SPREAD_STEP = 4
 SPREAD_ROW0 = 1
 ROW_IN_PLACE = 1
@@ -36,6 +36,7 @@ X_PLANE = (8, 12)
 GATHERS = ((128, 384, 512), (128, 128, 128, 128, 128, 128, 128, 128))
 LEAD_STATIONARY_CODES, LEAD_STATIONARY_SCALES, LEAD_MOVING_CODES, LEAD_MOVING_SCALES = 64, 0, 128, 192
 CHUNKS = ((0, 256, (0,)), (256, 256, (1, 2)), (512, 256, (3, 4)), (768, 128, (5,)), (896, 128, (0, 6)))
+WARM_PASSES = (512, 512, 256)
 H_COL0 = (0, 256, 0, 256, 384)
 
 
@@ -47,11 +48,11 @@ def tile_picked_zskip_silu_p_kernel(
         keep = ctx.enter_context(tc.tile_pool(name="keep", bufs=1))
         psum = ctx.enter_context(tc.psum_pool(name="psum", bufs=1))
 
-        def sb(name, shape, dtype, tag=None):
-            return keep.tile(shape, dtype, name=name, tag=tag or name, align_bytes=256)
+        def sb(name, shape, dtype):
+            return keep.tile(shape, dtype, name=name, align_bytes=256)
 
-        def bytes_at(name, width, lead, tag=None):
-            return sb(name, [P, lead + width], U8, tag)[:, lead:]
+        def bytes_at(name, width, lead):
+            return sb(name, [P, lead + width], U8)[:, lead:]
 
         def words_at(name, width, lead):
             return sb(name, [P, lead // PACK + width], U32)[:, lead // PACK :]
@@ -59,7 +60,7 @@ def tile_picked_zskip_silu_p_kernel(
         offsets = sb("offsets", [P, S // LIST_ROWS], U16)
         xs_table = sb("xs_table", [P, T], U8)
         xs_picked = sb("xs_picked", [P, S], U8)
-        xs = [bytes_at("xs0", S, LEAD_MOVING_SCALES)]
+        xs = [bytes_at("xs%d" % g, S, LEAD_MOVING_SCALES) for g in range(PASSES)]
         ws = bytes_at("ws", (PASSES + 1) * N, LEAD_STATIONARY_SCALES)
         w1_raw = [sb("w1_raw%d" % g, [P, PACK, H], F32) for g in range(PASSES)]
         w1_bf = [sb("w1_bf%d" % g, [P, PACK, P, PACK], BF16) for g in range(PASSES)]
@@ -142,18 +143,32 @@ def tile_picked_zskip_silu_p_kernel(
         move_scales(0)
         load_w1(1, W1_FIRST[1], PACK * H)
         load_x(1)
-        round_w1(0)
-        xs.append(bytes_at("xs1", S, LEAD_MOVING_SCALES, "w1_raw0"))
         copy_scales(1)
+        round_w1(0)
         quantize_w1(0)
         move_scales(1)
-        for r in range(QUAD_ROWS - 1):
-            load_w2_scales(r)
+        load_w3_scales(0)
+        load_w3_scales(1)
         nc.sync.dma_start(w23[:, :PASSES, :], w3_words.rearrange("g p n t -> p g (n t)").bitcast(I32))
-        load_w2_scales(QUAD_ROWS - 1)
+        load_w2_scales(0)
+        load_w2_scales(1)
         nc.sync.dma_start(w23[:, PASSES, :], w2_words[0].rearrange("p n t -> p (n t)").bitcast(I32))
-        for r in range(QUAD_ROWS):
-            load_w3_scales(r)
+        load_w2_scales(2)
+        load_w2_scales(3)
+        load_w3_scales(2)
+        load_w3_scales(3)
+
+        for i, width in enumerate(WARM_PASSES):
+            unread = psum.tile([P, BANK_COLS], F32, name="unread%d" % i, tag="bank%d" % (BANKS - 1 - i))
+            nc.tensor.matmul_mx(
+                out=unread[:, :width],
+                lhsT=w1_codes[0][:, :P].bitcast(FP8X4),
+                lhsT_scale=w1_scales[0][:, :P],
+                rhs=w1_codes[0][:, :width].bitcast(FP8X4),
+                rhs_scale=w1_scales[0][:, :width],
+                start=True,
+                stop=True,
+            )
 
         hidden = [psum.tile([P, BANK_COLS], F32, name="h%d" % b, tag="bank%d" % b) for b in range(BANKS)]
 

@@ -27,13 +27,13 @@ BANK_COLS = 512
 BANK_TOKENS = S // BANKS
 HALVES = N // P
 
-VECTOR_SHARE = (44, 64)
-W1_FIRST = (384, 1408)
+VECTOR_SHARE = (48, 64)
+W1_FIRST = (256, 1408)
 SPREAD_STEP = 4
 SPREAD_ROW0 = 1
 ROW_IN_PLACE = 1
 X_PLANE = (8, 12)
-GATHERS = ((128, 384, 512), (128, 128, 128, 128, 128, 128, 128, 128))
+GATHERS = ((384, 640), (128, 128, 128, 128, 128, 128, 128, 128))
 LEAD_STATIONARY_CODES, LEAD_STATIONARY_SCALES, LEAD_MOVING_CODES, LEAD_MOVING_SCALES = 64, 0, 128, 192
 CHUNKS = ((0, 256, (0,)), (256, 256, (1, 2)), (512, 256, (3, 4)), (768, 128, (5,)), (896, 128, (0, 6)))
 WARM_PASSES = (512, 512, 256)

@@ -27,8 +27,8 @@ BANK_COLS = 512
 BANK_TOKENS = S // BANKS
 HALVES = N // P
 
-VECTOR_SHARE = (48, 64)
-W1_FIRST = (256, 1408)
+VECTOR_SHARE = (44, 64)
+W1_FIRST = (320, 1536)
 SPREAD_STEP = 4
 SPREAD_ROW0 = 1
 ROW_IN_PLACE = 1

from contextlib import ExitStack

import concourse.mybir as mybir

K, T, S, H, N = 1024, 2048, 1024, 512, 256
FLOPS = 2 * S * (K * H + H * N + K * N)

F32 = mybir.dt.float32
BF16 = mybir.dt.bfloat16
I32 = mybir.dt.int32
U32 = mybir.dt.uint32
U16 = mybir.dt.uint16
U8 = mybir.dt.uint8
FP8X4 = mybir.dt.float8_e4m3fn_x4
SILU = mybir.ActivationFunctionType.Silu

P = 128
PACK = 4
PASS_K = P * PACK
PASSES = K // PASS_K
QUADS = 4
QUAD = P // QUADS
QUAD_ROWS = 4
LIST_ROWS = 16
BANKS = 8
BANK_COLS = 512
BANK_TOKENS = S // BANKS
HALVES = N // P

VECTOR_SHARE = (44, 64)
W1_FIRST = (320, 1536)
SPREAD_STEP = 4
SPREAD_ROW0 = 1
ROW_IN_PLACE = 1
X_PLANE = (8, 12)
GATHERS = ((384, 640), (128, 128, 128, 128, 128, 128, 128, 128))
LEAD_STATIONARY_CODES, LEAD_STATIONARY_SCALES, LEAD_MOVING_CODES, LEAD_MOVING_SCALES = 64, 0, 128, 192
CHUNKS = ((0, 256, (0,)), (256, 256, (1, 2)), (512, 256, (3, 4)), (768, 128, (5,)), (896, 128, (0, 6)))
WARM_PASSES = (512, 512, 256)
H_COL0 = (0, 256, 0, 256, 384)


def tile_picked_zskip_silu_p_kernel(
    tc, x_words, x_scales, w1, w2_words, w2_scales, w3_words, w3_scales, offs, out
):
    nc = tc.nc
    with ExitStack() as ctx:
        keep = ctx.enter_context(tc.tile_pool(name="keep", bufs=1))
        psum = ctx.enter_context(tc.psum_pool(name="psum", bufs=1))

        def sb(name, shape, dtype):
            return keep.tile(shape, dtype, name=name, align_bytes=256)

        def bytes_at(name, width, lead):
            return sb(name, [P, lead + width], U8)[:, lead:]

        def words_at(name, width, lead):
            return sb(name, [P, lead // PACK + width], U32)[:, lead // PACK :]

        offsets = sb("offsets", [P, S // LIST_ROWS], U16)
        xs_table = sb("xs_table", [P, T], U8)
        xs_picked = sb("xs_picked", [P, S], U8)
        xs = [bytes_at("xs%d" % g, S, LEAD_MOVING_SCALES) for g in range(PASSES)]
        ws = bytes_at("ws", (PASSES + 1) * N, LEAD_STATIONARY_SCALES)
        w1_raw = [sb("w1_raw%d" % g, [P, PACK, H], F32) for g in range(PASSES)]
        w1_bf = [sb("w1_bf%d" % g, [P, PACK, P, PACK], BF16) for g in range(PASSES)]
        w1_codes = [words_at("w1_codes%d" % g, H, LEAD_STATIONARY_CODES) for g in range(PASSES)]
        w1_scales = [bytes_at("w1_scales%d" % g, H, LEAD_STATIONARY_SCALES) for g in range(PASSES)]
        x_table = [sb("x_table%d" % g, [P, T], I32) for g in range(PASSES)]
        x_codes = [words_at("x_codes%d" % g, S, LEAD_MOVING_CODES) for g in range(PASSES)]
        w23_row = sb("w23", [P, LEAD_STATIONARY_CODES // PACK + (PASSES + 1) * N], I32)[:, LEAD_STATIONARY_CODES // PACK :]
        w23 = w23_row.rearrange("p (g n) -> p g n", n=N)
        h_bf = [sb("h_bf%d" % c, [P, width, PACK], BF16) for c, (tok0, width, banks) in enumerate(CHUNKS)]
        h_codes = words_at("h_codes", S, LEAD_MOVING_CODES)
        h_scales = bytes_at("h_scales", S, LEAD_MOVING_SCALES)

        nc.vector.memset(xs_table[:].bitcast(I32), 0)

        warm = sb("warm", [P, 16], F32)
        warm_out = sb("warm_out", [P, 16], F32)
        nc.vector.memset(warm[:], 0.0)
        nc.scalar.activation(warm_out[:], warm[:], SILU)

        nc.vector.memset(ws.bitcast(I32), 0)

        def load_w1(g, v0, v1):
            rows = w1[PASS_K * g : PASS_K * (g + 1), :].rearrange("(p j) c -> p (j c)", j=PACK)
            nc.sync.dma_start(w1_raw[g][:].rearrange("p j c -> p (j c)")[:, v0:v1], rows[:, v0:v1])

        def load_x(g):
            nc.sync.dma_start(x_table[g][:], x_words[g].rearrange("p n t -> p (n t)").bitcast(I32))

        def copy_scales(g):
            nc.vector.tensor_copy(xs[g].bitcast(I32), xs_picked[:].bitcast(I32))

        def move_scales(g):
            for r in range(QUAD_ROWS):
                if r != ROW_IN_PLACE:
                    src = SPREAD_ROW0 + SPREAD_STEP * (PASSES * r + g)
                    nc.sync.dma_start(
                        xs[g][X_PLANE[g] + r : P : QUAD, :].bitcast(I32), xs_picked[src:P:QUAD, :].bitcast(I32)
                    )

        def round_w1(g):
            dst = w1_bf[g][:].rearrange("p t m j -> p m j t")
            src = w1_raw[g][:].rearrange("p j (m t) -> p m j t", t=PACK)
            nc.scalar.copy(dst[:, VECTOR_SHARE[g] :], src[:, VECTOR_SHARE[g] :])
            nc.vector.tensor_copy(dst[:, : VECTOR_SHARE[g]], src[:, : VECTOR_SHARE[g]])

        def quantize_w1(g):
            nc.vector.quantize_mx(
                out=w1_codes[g].bitcast(FP8X4),
                scales=w1_scales[g],
                in_=w1_bf[g][:].rearrange("p t m j -> p (t m j)"),
            )

        def gather_words(g):
            tok0 = 0
            for width in GATHERS[g]:
                entries = offsets[:, tok0 // LIST_ROWS : (tok0 + width) // LIST_ROWS]
                nc.vector.tensor_copy(x_codes[g][:, tok0 : tok0 + width], x_table[g][:].bitcast(U32).indirect(entries))
                tok0 = tok0 + width

        def load_w2_scales(r):
            nc.sync.dma_start(ws[r:P:QUAD, PASSES * N :].bitcast(I32), w2_scales[0, r::QUAD_ROWS, :].bitcast(I32))

        def load_w3_scales(r):
            nc.sync.dma_start(
                ws[r:P:QUAD, : PASSES * N].bitcast(I32).rearrange("q (g n) -> q g n", g=PASSES),
                w3_scales[:, r::QUAD_ROWS, :].bitcast(I32).rearrange("g q n -> q g n"),
            )

        load_w1(0, 0, W1_FIRST[0])
        nc.sync.dma_start(offsets[:], offs)
        nc.sync.dma_start(
            xs_table[SPREAD_ROW0:P:SPREAD_STEP, :].bitcast(I32), x_scales.rearrange("g q n -> q g n").bitcast(I32)
        )
        load_w1(0, W1_FIRST[0], PACK * H)
        load_x(0)
        nc.vector.tensor_copy(xs_picked[:], xs_table[:].indirect(offsets[:]))
        copy_scales(0)
        load_w1(1, 0, W1_FIRST[1])
        move_scales(0)
        load_w1(1, W1_FIRST[1], PACK * H)
        load_x(1)
        copy_scales(1)
        round_w1(0)
        quantize_w1(0)
        move_scales(1)
        load_w3_scales(0)
        load_w3_scales(1)
        nc.sync.dma_start(w23[:, :PASSES, :], w3_words.rearrange("g p n t -> p g (n t)").bitcast(I32))
        load_w2_scales(0)
        load_w2_scales(1)
        nc.sync.dma_start(w23[:, PASSES, :], w2_words[0].rearrange("p n t -> p (n t)").bitcast(I32))
        load_w2_scales(2)
        load_w2_scales(3)
        load_w3_scales(2)
        load_w3_scales(3)

        for i, width in enumerate(WARM_PASSES):
            unread = psum.tile([P, BANK_COLS], F32, name="unread%d" % i, tag="bank%d" % (BANKS - 1 - i))
            nc.tensor.matmul_mx(
                out=unread[:, :width],
                lhsT=w1_codes[0][:, :P].bitcast(FP8X4),
                lhsT_scale=w1_scales[0][:, :P],
                rhs=w1_codes[0][:, :width].bitcast(FP8X4),
                rhs_scale=w1_scales[0][:, :width],
                start=True,
                stop=True,
            )

        hidden = [psum.tile([P, BANK_COLS], F32, name="h%d" % b, tag="bank%d" % b) for b in range(BANKS)]

        def hidden_pass(g, b):
            tokens = slice(BANK_TOKENS * b, BANK_TOKENS * (b + 1))
            for t in range(PACK):
                tile_cols = slice(P * t, P * (t + 1))
                nc.tensor.matmul_mx(
                    out=hidden[b][:, tile_cols],
                    lhsT=w1_codes[g][:, tile_cols].bitcast(FP8X4),
                    lhsT_scale=w1_scales[g][:, tile_cols],
                    rhs=x_codes[g][:, tokens].bitcast(FP8X4),
                    rhs_scale=xs[g][X_PLANE[g] : P, tokens],
                    start=(g == 0 and t == 0),
                    stop=(g == PASSES - 1 and t == PACK - 1),
                )

        def silu(b):
            c = max(i for i, chunk in enumerate(CHUNKS) if chunk[0] <= BANK_TOKENS * b)
            n0 = BANK_TOKENS * b - CHUNKS[c][0]
            nc.scalar.activation(
                h_bf[c][:, n0 : n0 + BANK_TOKENS, :], hidden[b][:].rearrange("p (t n) -> p n t", t=PACK), SILU
            )

        gather_words(0)
        for b in range(BANKS):
            hidden_pass(0, b)
        round_w1(1)
        quantize_w1(1)

        out_halves = out.rearrange("(m p) n -> p m n", p=P)
        sums = {}
        result = [sb("result%d" % c, [P, HALVES, width], F32) for c, (tok0, width, banks) in enumerate(CHUNKS)]

        def tokens_of(c):
            return slice(CHUNKS[c][0], CHUNKS[c][0] + CHUNKS[c][1])

        def h_cols(c):
            return slice(H_COL0[c], H_COL0[c] + CHUNKS[c][1])

        def quantize_h(c, n0, n1):
            cols = slice(H_COL0[c] + n0, H_COL0[c] + n1)
            nc.vector.quantize_mx(
                out=h_codes[:, cols].bitcast(FP8X4),
                scales=h_scales[:, cols],
                in_=h_bf[c][:, n0:n1, :].rearrange("p n t -> p (n t)"),
            )

        def open_sums(c):
            tok0, width, banks = CHUNKS[c]
            tiles = [psum.tile([P, BANK_COLS], F32, name="o%d_%d" % (c, b), tag="bank%d" % b) for b in banks]
            if len(banks) == HALVES:
                sums[c] = [tile[:, :width] for tile in tiles]
            else:
                sums[c] = [tiles[0][:, width * m : width * (m + 1)] for m in range(HALVES)]
                sums[c].append(tiles[0][:, : HALVES * width].rearrange("p (m n) -> p m n", m=HALVES))

        def shortcut(c, m):
            for g in range(PASSES):
                nc.tensor.matmul_mx(
                    out=sums[c][m],
                    lhsT=w23[:, g, P * m : P * (m + 1)].bitcast(FP8X4),
                    lhsT_scale=ws[:, N * g + P * m : N * g + P * (m + 1)],
                    rhs=x_codes[g][:, tokens_of(c)].bitcast(FP8X4),
                    rhs_scale=xs[g][X_PLANE[g] : P, tokens_of(c)],
                    start=(g == 0 and m < len(CHUNKS[c][2])),
                    stop=False,
                )

        def close(c, m):
            nc.tensor.matmul_mx(
                out=sums[c][m],
                lhsT=w23[:, PASSES, P * m : P * (m + 1)].bitcast(FP8X4),
                lhsT_scale=ws[:, PASSES * N + P * m : PASSES * N + P * (m + 1)],
                rhs=h_codes[:, h_cols(c)].bitcast(FP8X4),
                rhs_scale=h_scales[:, h_cols(c)],
                start=False,
                stop=(m >= HALVES - len(CHUNKS[c][2])),
            )

        def products_half_by_half(c):
            open_sums(c)
            for m in range(HALVES):
                shortcut(c, m)
                close(c, m)

        def products_shortcuts_first(c):
            open_sums(c)
            for m in range(HALVES):
                shortcut(c, m)
            for m in range(HALVES):
                close(c, m)

        def store_whole(c, copy):
            copy(result[c][:], sums[c][HALVES])
            nc.sync.dma_start(out_halves[:, :, tokens_of(c)], result[c][:])

        def store_half(c, m, copy):
            copy(result[c][:, m, :], sums[c][m])
            nc.sync.dma_start(out_halves[:, m, tokens_of(c)], result[c][:, m, :])

        gather_words(1)
        for b in range(BANKS):
            hidden_pass(1, b)
            silu(b)
        quantize_h(0, 0, 256)
        quantize_h(1, 0, 256)
        products_shortcuts_first(0)
        store_whole(0, nc.vector.tensor_copy)
        quantize_h(2, 0, 256)
        products_shortcuts_first(1)
        for m in range(HALVES):
            store_half(1, m, nc.vector.tensor_copy)
        quantize_h(3, 0, 128)
        products_shortcuts_first(2)
        store_half(2, 0, nc.scalar.copy)
        quantize_h(4, 0, 128)
        store_half(2, 1, nc.vector.tensor_copy)
        products_shortcuts_first(3)
        store_whole(3, nc.scalar.copy)
        products_half_by_half(4)
        store_half(4, 0, nc.vector.tensor_copy)
        store_half(4, 1, nc.scalar.copy)
